import numpy as np
import ml_dtypes


def mxq(x, axis, fmt="e4m3"):
    dtype, down = {"e4m3": (ml_dtypes.float8_e4m3fn, 7), "e5m2": (ml_dtypes.float8_e5m2, 14)}[fmt]
    v = np.moveaxis(np.asarray(x, np.float32).astype(ml_dtypes.bfloat16).astype(np.float64), axis, -1)
    blocks = v.reshape(v.shape[:-1] + (-1, 32))
    amax = np.abs(blocks).max(-1, keepdims=True)
    byte = np.maximum(np.where(amax > 0, np.frexp(amax)[1] - 1 + 127, 0) - down, 1)
    scale = np.exp2(byte - 127.0)
    codes = (blocks / scale).astype(np.float32).astype(dtype).astype(np.float64)
    return np.moveaxis((codes * scale).reshape(v.shape), -1, axis)


WIDE = False


def mx_kscale(k):
    if not WIDE:
        return np.ones(k)
    levels = np.array([10, -10, 5, -5, 0])
    if k % 512:
        return np.exp2(np.random.permutation(np.resize(levels, k // 32))).repeat(32)
    a = np.empty((k // 512, 16))
    for p in range(k // 512):
        a[p, :8] = np.random.permutation(np.resize(levels, 8))
        for g in range(8):
            far = levels[np.abs(levels - a[p, g]) >= 10]
            a[p, g + 8] = far[np.random.randint(len(far))]
    return np.exp2(a.ravel()).repeat(32)


def f64(x):
    return np.asarray(x).astype(np.float64)


def striped(idx):
    return np.tile(idx.reshape(-1, 16).T, (8, 1)).astype(np.uint16)


def unstriped(offs):
    return offs[:16].T.reshape(-1).astype(np.int64)


def pack_weight(w):
    k, n = w.shape
    w = f64(np.asarray(w, np.float32).astype(ml_dtypes.bfloat16)).reshape(k // 32, 32, n)
    amax = np.abs(w).max(1)
    byte = np.clip(np.where(amax > 0, np.frexp(amax)[1] - 1 + 127 - 7, 1), 1, 254)
    scaled = (w * np.exp2(127.0 - byte)[:, None, :]).reshape(k, n).astype(np.float32)
    words = np.ascontiguousarray(scaled.reshape(k // 512, 128, 4, n).transpose(0, 1, 3, 2)).astype(ml_dtypes.float8_e4m3fn).view(np.uint8)
    return words, np.ascontiguousarray(byte.astype(np.uint8).reshape(k // 512, 16, n))


def unpack_weight(words, scales):
    g, p, n, _ = words.shape
    vals = np.ascontiguousarray(words).view(ml_dtypes.float8_e4m3fn).astype(np.float64) * np.repeat(np.exp2(scales.astype(np.float64) - 127.0), 8, axis=1)[..., None]
    return vals.transpose(0, 1, 3, 2).reshape(g * 512, n)


K, T, S, H, N, U = 512, 2048, 512, 512, 256, 1024


def setup_inputs():
    n = np.random.standard_normal
    s = mx_kscale(K)[:, None]
    u = mx_kscale(H)
    packed_w2 = pack_weight(n((H, N)) / np.sqrt(H) / u[:, None])
    return {
        "xT": (n((K, T)) * s).astype(np.float32),
        "w1": (n((K, H)) / np.sqrt(K) / s * u).astype(np.float32),
        "w2_words": packed_w2[0],
        "w2_scales": packed_w2[1],
        "skip": (n((H, U)) * u[:, None]).astype(np.float32),
        "offs": striped(np.random.permutation(T)[:S]),
        "cell": striped(np.random.permutation(U)[:S]),
    }


def reference(xT, w1, w2_words, w2_scales, skip, offs, cell):
    xq = mxq(f64(xT)[:, unstriped(offs)], 0, "e4m3")
    up = np.zeros((H, U))
    up[:, unstriped(cell)] = mxq(f64(w1), 0, "e4m3").T @ xq
    z = up + f64(skip)
    return unpack_weight(w2_words, w2_scales).T @ mxq(z, 0, "e4m3")

@@ -1,0 +1,164 @@
+from contextlib import ExitStack
+
+import concourse.mybir as mybir
+
+K, T, S, H, N, U = 512, 2048, 512, 512, 256, 1024
+FLOPS = 2 * K * H * S + 2 * H * N * U
+
+F32 = mybir.dt.float32
+BF16 = mybir.dt.bfloat16
+I32 = mybir.dt.int32
+U32 = mybir.dt.uint32
+U16 = mybir.dt.uint16
+U8 = mybir.dt.uint8
+FP8X4 = mybir.dt.float8_e4m3fn_x4
+ADD = mybir.AluOpType.add
+
+P = 128
+PACK = 4
+BANK = 512
+HALF = S // 2
+CELL_CHUNKS = (256, 256, 256, 128, 128)
+
+
+def tile_picked_unet_none_e_kernel(
+    tc, xT, w1, w2_words, w2_scales, skip, offs, cell, out
+):
+    nc = tc.nc
+    with ExitStack() as ctx:
+        keep = ctx.enter_context(tc.tile_pool(name="keep", bufs=1))
+        psum = ctx.enter_context(tc.psum_pool(name="psum", bufs=8))
+
+        offs_sb = keep.tile([P, S // 16], U16, name="offs_sb")
+        cell_sb = keep.tile([P, S // 16], U16, name="cell_sb")
+        nc.sync.dma_start(offs_sb[:], offs)
+
+        w1_raw = keep.tile([P, PACK, H], F32, name="w1_raw")
+        nc.sync.dma_start(w1_raw[:], w1.rearrange("(p j) c -> p j c", j=PACK))
+        x_rows = xT.rearrange("(p j) t -> p j t", j=PACK)
+        x_raw = []
+        for j in range(PACK):
+            plane = keep.tile([P, T], F32, name="x_raw%d" % j)
+            nc.sync.dma_start(plane[:], x_rows[:, j, :])
+            x_raw.append(plane)
+        nc.sync.dma_start(cell_sb[:], cell)
+        skip_rows = skip.rearrange("(p t) v -> p t v", t=PACK)
+        skip_sb = []
+        for t in range(PACK):
+            plane = keep.tile([P, U], F32, name="skip_sb%d" % t)
+            nc.sync.dma_start(plane[:], skip_rows[:, t, :])
+            skip_sb.append(plane)
+        w2_codes = keep.tile([P, N], I32, name="w2_codes", align_bytes=64)
+        nc.sync.dma_start(w2_codes[:], w2_words[0].rearrange("p n r -> p (n r)").bitcast(I32))
+        w2_sc = keep.tile([P, N], U8, name="w2_sc", align_bytes=64)
+        nc.vector.memset(w2_sc[:].bitcast(I32), 0)
+        for q in range(4):
+            nc.sync.dma_start(w2_sc[32 * q : 32 * q + 4, :].bitcast(I32), w2_scales[0, 4 * q : 4 * q + 4, :].bitcast(I32))
+
+        up = []
+        for t in range(PACK):
+            window = keep.tile([P, U], F32, name="up%d" % t)
+            nc.vector.memset(window[:], 0.0)
+            up.append(window)
+
+        w1_bf = keep.tile([P, H * PACK], BF16, name="w1_bf", align_bytes=64)
+        nc.scalar.copy(
+            w1_bf[:].rearrange("p (t m j) -> p t m j", t=PACK, j=PACK),
+            w1_raw[:].rearrange("p j (m t) -> p t m j", t=PACK),
+        )
+        w1_codes = keep.tile([P, H], U32, name="w1_codes", align_bytes=64)
+        w1_sc = keep.tile([P, H], U8, name="w1_sc", align_bytes=64)
+        nc.vector.quantize_mx(out=w1_codes[:].bitcast(FP8X4), scales=w1_sc[:], in_=w1_bf[:])
+
+        halves = [slice(a * HALF, (a + 1) * HALF) for a in range(2)]
+        list_halves = [slice(a * HALF // 16, (a + 1) * HALF // 16) for a in range(2)]
+        x_bf = keep.tile([P, S, PACK], BF16, name="x_bf", align_bytes=64)
+        for j in range(PACK - 1):
+            nc.vector.tensor_copy(x_bf[:, :, j], x_raw[j][:].indirect(offs_sb[:]))
+        x_codes = keep.tile([P, S], U32, name="x_codes", align_bytes=64)
+        x_sc = keep.tile([P, S], U8, name="x_sc", align_bytes=64)
+        for a in range(2):
+            nc.vector.tensor_copy(x_bf[:, halves[a], PACK - 1], x_raw[PACK - 1][:].indirect(offs_sb[:, list_halves[a]]))
+        for a in range(2):
+            nc.vector.quantize_mx(
+                out=x_codes[:, halves[a]].bitcast(FP8X4),
+                scales=x_sc[:, halves[a]],
+                in_=x_bf[:, halves[a], :].rearrange("p s j -> p (s j)"),
+            )
+
+        h = [keep.tile([P, S], F32, name="h%d" % t) for t in range(PACK)]
+
+        def first_layer(t, cols):
+            width = cols.stop - cols.start
+            bank = psum.tile([P, BANK], F32, name="bank")
+            nc.tensor.matmul_mx(
+                out=bank[:, :width],
+                lhsT=w1_codes[:, t * P : (t + 1) * P].bitcast(FP8X4),
+                lhsT_scale=w1_sc[:, t * P : (t + 1) * P],
+                rhs=x_codes[:, cols].bitcast(FP8X4),
+                rhs_scale=x_sc[:, cols],
+                start=True,
+                stop=True,
+            )
+            nc.scalar.copy(h[t][:, cols], bank[:, :width])
+
+        for a in range(2):
+            for t in range(2):
+                first_layer(t, halves[a])
+        for t in range(2, PACK):
+            first_layer(t, slice(0, S))
+
+        z_pair = [keep.tile([P, 2, U], BF16, name="z_pair%d" % u) for u in range(2)]
+        for a in range(2):
+            for t in range(2):
+                nc.vector.tensor_copy(up[t][:].indirect(cell_sb[:, list_halves[a]]), h[t][:, halves[a]])
+        for t in range(2):
+            nc.vector.tensor_tensor(z_pair[0][:, t, :], up[t][:], skip_sb[t][:], ADD)
+        nc.vector.tensor_copy(up[2][:].indirect(cell_sb[:]), h[2][:])
+        nc.vector.tensor_tensor(z_pair[1][:, 0, :], up[2][:], skip_sb[2][:], ADD)
+        nc.vector.tensor_copy(up[3][:].indirect(cell_sb[:]), h[3][:])
+
+        starts = [sum(CELL_CHUNKS[:c]) for c in range(len(CELL_CHUNKS))]
+        chunks = [slice(s, s + w) for s, w in zip(starts, CELL_CHUNKS)]
+        z_bf = [keep.tile([P, w, PACK], BF16, name="z_bf%d" % c, align_bytes=64) for c, w in enumerate(CELL_CHUNKS)]
+        for c, cols in enumerate(chunks):
+            nc.scalar.copy(z_bf[c][:, :, 0:2], z_pair[0][:, :, cols].rearrange("p e v -> p v e"))
+
+        out_rows = out.rearrange("(g p) v -> p g v", p=P)
+
+        def add_last(c):
+            nc.vector.tensor_tensor(z_pair[1][:, 1, chunks[c]], up[3][:, chunks[c]], skip_sb[3][:, chunks[c]], ADD)
+
+        def weave(c):
+            nc.vector.tensor_copy(z_bf[c][:, :, 2:4], z_pair[1][:, :, chunks[c]].rearrange("p e v -> p v e"))
+
+        def second_layer(c):
+            width = CELL_CHUNKS[c]
+            z_codes = keep.tile([P, width], U32, name="z_codes%d" % c, align_bytes=64)
+            z_sc = keep.tile([P, width], U8, name="z_sc%d" % c, align_bytes=64)
+            nc.vector.quantize_mx(
+                out=z_codes[:].bitcast(FP8X4), scales=z_sc[:], in_=z_bf[c][:].rearrange("p v t -> p (v t)")
+            )
+            bank = psum.tile([P, BANK], F32, name="bank")
+            for g in range(2):
+                nc.tensor.matmul_mx(
+                    out=bank[:, g * width : (g + 1) * width],
+                    lhsT=w2_codes[:, g * P : (g + 1) * P].bitcast(FP8X4),
+                    lhsT_scale=w2_sc[:, g * P : (g + 1) * P],
+                    rhs=z_codes[:].bitcast(FP8X4),
+                    rhs_scale=z_sc[:],
+                    start=True,
+                    stop=True,
+                )
+            res = keep.tile([P, 2, width], F32, name="res%d" % c)
+            nc.scalar.copy(res[:].rearrange("p g v -> p (g v)"), bank[:, : 2 * width])
+            nc.sync.dma_start(out_rows[:, :, chunks[c]], res[:])
+
+        n = len(CELL_CHUNKS)
+        for step in range(n + 2):
+            if step < n:
+                add_last(step)
+            if 1 <= step <= n:
+                weave(step - 1)
+            if step >= 2:
+                second_layer(step - 2)

@@ -18,7 +18,7 @@ P = 128
 PACK = 4
 BANK = 512
 HALF = S // 2
-CELL_CHUNKS = (256, 256, 256, 128, 128)
+CELL_CHUNKS = (128, 256, 256, 128, 128, 128)
 
 
 def tile_picked_unet_none_e_kernel(
@@ -31,16 +31,21 @@ def tile_picked_unet_none_e_kernel(
 
         offs_sb = keep.tile([P, S // 16], U16, name="offs_sb")
         cell_sb = keep.tile([P, S // 16], U16, name="cell_sb")
-        nc.sync.dma_start(offs_sb[:], offs)
 
-        w1_raw = keep.tile([P, PACK, H], F32, name="w1_raw")
-        nc.sync.dma_start(w1_raw[:], w1.rearrange("(p j) c -> p j c", j=PACK))
         x_rows = xT.rearrange("(p j) t -> p j t", j=PACK)
         x_raw = []
         for j in range(PACK):
             plane = keep.tile([P, T], F32, name="x_raw%d" % j)
             nc.sync.dma_start(plane[:], x_rows[:, j, :])
             x_raw.append(plane)
+            if j == 0:
+                nc.sync.dma_start(offs_sb[:], offs)
+        w1_rows = w1.rearrange("(p j) c -> p j c", j=PACK)
+        w1_raw = []
+        for b in range(2):
+            part = keep.tile([P, PACK, H // 2], F32, name="w1_raw%d" % b)
+            nc.sync.dma_start(part[:], w1_rows[:, :, b * (H // 2) : (b + 1) * (H // 2)])
+            w1_raw.append(part)
         nc.sync.dma_start(cell_sb[:], cell)
         skip_rows = skip.rearrange("(p t) v -> p t v", t=PACK)
         skip_sb = []
@@ -61,30 +66,26 @@ def tile_picked_unet_none_e_kernel(
             nc.vector.memset(window[:], 0.0)
             up.append(window)
 
-        w1_bf = keep.tile([P, H * PACK], BF16, name="w1_bf", align_bytes=64)
-        nc.scalar.copy(
-            w1_bf[:].rearrange("p (t m j) -> p t m j", t=PACK, j=PACK),
-            w1_raw[:].rearrange("p j (m t) -> p t m j", t=PACK),
-        )
-        w1_codes = keep.tile([P, H], U32, name="w1_codes", align_bytes=64)
-        w1_sc = keep.tile([P, H], U8, name="w1_sc", align_bytes=64)
-        nc.vector.quantize_mx(out=w1_codes[:].bitcast(FP8X4), scales=w1_sc[:], in_=w1_bf[:])
-
         halves = [slice(a * HALF, (a + 1) * HALF) for a in range(2)]
         list_halves = [slice(a * HALF // 16, (a + 1) * HALF // 16) for a in range(2)]
         x_bf = keep.tile([P, S, PACK], BF16, name="x_bf", align_bytes=64)
-        for j in range(PACK - 1):
+        for j in range(PACK):
             nc.vector.tensor_copy(x_bf[:, :, j], x_raw[j][:].indirect(offs_sb[:]))
         x_codes = keep.tile([P, S], U32, name="x_codes", align_bytes=64)
         x_sc = keep.tile([P, S], U8, name="x_sc", align_bytes=64)
-        for a in range(2):
-            nc.vector.tensor_copy(x_bf[:, halves[a], PACK - 1], x_raw[PACK - 1][:].indirect(offs_sb[:, list_halves[a]]))
-        for a in range(2):
-            nc.vector.quantize_mx(
-                out=x_codes[:, halves[a]].bitcast(FP8X4),
-                scales=x_sc[:, halves[a]],
-                in_=x_bf[:, halves[a], :].rearrange("p s j -> p (s j)"),
-            )
+        nc.vector.quantize_mx(out=x_codes[:].bitcast(FP8X4), scales=x_sc[:], in_=x_bf[:].rearrange("p s j -> p (s j)"))
+
+        w1_bf = [keep.tile([P, 2 * P * PACK], BF16, name="w1_bf%d" % u, align_bytes=64) for u in range(2)]
+        w1_codes = [keep.tile([P, 2 * P], U32, name="w1_codes%d" % u, align_bytes=64) for u in range(2)]
+        w1_sc = [keep.tile([P, 2 * P], U8, name="w1_sc%d" % u, align_bytes=64) for u in range(2)]
+        for b in range(2):
+            for u in range(2):
+                nc.scalar.copy(
+                    w1_bf[u][:].rearrange("p (e b mm mi j) -> p b mm j mi e", e=2, b=2, mi=2, j=PACK)[:, b],
+                    w1_raw[b][:].rearrange("p j (mm mi u e) -> p u mm j mi e", mi=2, u=2, e=2)[:, u],
+                )
+        for u in range(2):
+            nc.vector.quantize_mx(out=w1_codes[u][:].bitcast(FP8X4), scales=w1_sc[u][:], in_=w1_bf[u][:])
 
         h = [keep.tile([P, S], F32, name="h%d" % t) for t in range(PACK)]
 
@@ -93,8 +94,8 @@ def tile_picked_unet_none_e_kernel(
             bank = psum.tile([P, BANK], F32, name="bank")
             nc.tensor.matmul_mx(
                 out=bank[:, :width],
-                lhsT=w1_codes[:, t * P : (t + 1) * P].bitcast(FP8X4),
-                lhsT_scale=w1_sc[:, t * P : (t + 1) * P],
+                lhsT=w1_codes[t // 2][:, (t % 2) * P : (t % 2 + 1) * P].bitcast(FP8X4),
+                lhsT_scale=w1_sc[t // 2][:, (t % 2) * P : (t % 2 + 1) * P],
                 rhs=x_codes[:, cols].bitcast(FP8X4),
                 rhs_scale=x_sc[:, cols],
                 start=True,
@@ -108,36 +109,40 @@ def tile_picked_unet_none_e_kernel(
         for t in range(2, PACK):
             first_layer(t, slice(0, S))
 
-        z_pair = [keep.tile([P, 2, U], BF16, name="z_pair%d" % u) for u in range(2)]
+        z_rows = keep.tile([P, 3, U], BF16, name="z_rows")
+        z_slot = (0, 2, 1, 2)
         for a in range(2):
             for t in range(2):
                 nc.vector.tensor_copy(up[t][:].indirect(cell_sb[:, list_halves[a]]), h[t][:, halves[a]])
-        for t in range(2):
-            nc.vector.tensor_tensor(z_pair[0][:, t, :], up[t][:], skip_sb[t][:], ADD)
+        nc.gpsimd.tensor_tensor(z_rows[:, z_slot[0], :], up[0][:], skip_sb[0][:], ADD)
+        cell_halves = [slice(a * U // 2, (a + 1) * U // 2) for a in range(2)]
+        for cols in cell_halves:
+            nc.gpsimd.tensor_tensor(z_rows[:, z_slot[1], cols], up[1][:, cols], skip_sb[1][:, cols], ADD)
         nc.vector.tensor_copy(up[2][:].indirect(cell_sb[:]), h[2][:])
-        nc.vector.tensor_tensor(z_pair[1][:, 0, :], up[2][:], skip_sb[2][:], ADD)
+        nc.gpsimd.tensor_tensor(z_rows[:, z_slot[2], :], up[2][:], skip_sb[2][:], ADD)
         nc.vector.tensor_copy(up[3][:].indirect(cell_sb[:]), h[3][:])
 
         starts = [sum(CELL_CHUNKS[:c]) for c in range(len(CELL_CHUNKS))]
         chunks = [slice(s, s + w) for s, w in zip(starts, CELL_CHUNKS)]
-        z_bf = [keep.tile([P, w, PACK], BF16, name="z_bf%d" % c, align_bytes=64) for c, w in enumerate(CELL_CHUNKS)]
-        for c, cols in enumerate(chunks):
-            nc.scalar.copy(z_bf[c][:, :, 0:2], z_pair[0][:, :, cols].rearrange("p e v -> p v e"))
+        z_bf = keep.tile([P, U, PACK], BF16, name="z_bf", align_bytes=64)
+        for cols in cell_halves:
+            nc.scalar.copy(z_bf[:, cols, 0:2], z_rows[:, 0:3:2, cols].rearrange("p e v -> p v e"))
 
         out_rows = out.rearrange("(g p) v -> p g v", p=P)
 
         def add_last(c):
-            nc.vector.tensor_tensor(z_pair[1][:, 1, chunks[c]], up[3][:, chunks[c]], skip_sb[3][:, chunks[c]], ADD)
+            nc.vector.tensor_tensor(z_rows[:, z_slot[3], chunks[c]], up[3][:, chunks[c]], skip_sb[3][:, chunks[c]], ADD)
 
         def weave(c):
-            nc.vector.tensor_copy(z_bf[c][:, :, 2:4], z_pair[1][:, :, chunks[c]].rearrange("p e v -> p v e"))
+            move = nc.scalar.copy if c == 1 else nc.vector.tensor_copy
+            move(z_bf[:, chunks[c], 2:4], z_rows[:, 1:3, chunks[c]].rearrange("p e v -> p v e"))
 
         def second_layer(c):
             width = CELL_CHUNKS[c]
             z_codes = keep.tile([P, width], U32, name="z_codes%d" % c, align_bytes=64)
             z_sc = keep.tile([P, width], U8, name="z_sc%d" % c, align_bytes=64)
             nc.vector.quantize_mx(
-                out=z_codes[:].bitcast(FP8X4), scales=z_sc[:], in_=z_bf[c][:].rearrange("p v t -> p (v t)")
+                out=z_codes[:].bitcast(FP8X4), scales=z_sc[:], in_=z_bf[:, chunks[c], :].rearrange("p v t -> p (v t)")
             )
             bank = psum.tile([P, BANK], F32, name="bank")
             for g in range(2):
@@ -151,7 +156,8 @@ def tile_picked_unet_none_e_kernel(
                     stop=True,
                 )
             res = keep.tile([P, 2, width], F32, name="res%d" % c)
-            nc.scalar.copy(res[:].rearrange("p g v -> p (g v)"), bank[:, : 2 * width])
+            move = nc.vector.tensor_copy if c == len(CELL_CHUNKS) - 1 else nc.scalar.copy
+            move(res[:].rearrange("p g v -> p (g v)"), bank[:, : 2 * width])
             nc.sync.dma_start(out_rows[:, :, chunks[c]], res[:])
 
         n = len(CELL_CHUNKS)

@@ -18,7 +18,9 @@ P = 128
 PACK = 4
 BANK = 512
 HALF = S // 2
-CELL_CHUNKS = (128, 256, 256, 128, 128, 128)
+CELL_CHUNKS = (128, 256, 128, 256, 128, 128)
+W1_VECTOR_PAIRS = 40
+FIRST_PIECE = 128
 
 
 def tile_picked_unet_none_e_kernel(
@@ -40,18 +42,15 @@ def tile_picked_unet_none_e_kernel(
             x_raw.append(plane)
             if j == 0:
                 nc.sync.dma_start(offs_sb[:], offs)
-        w1_rows = w1.rearrange("(p j) c -> p j c", j=PACK)
-        w1_raw = []
-        for b in range(2):
-            part = keep.tile([P, PACK, H // 2], F32, name="w1_raw%d" % b)
-            nc.sync.dma_start(part[:], w1_rows[:, :, b * (H // 2) : (b + 1) * (H // 2)])
-            w1_raw.append(part)
+        w1_raw = keep.tile([P, PACK, H], F32, name="w1_raw")
+        nc.sync.dma_start(w1_raw[:], w1.rearrange("(p j) c -> p j c", j=PACK))
         nc.sync.dma_start(cell_sb[:], cell)
         skip_rows = skip.rearrange("(p t) v -> p t v", t=PACK)
         skip_sb = []
+        shared = keep.tile([P, U // 2 + U], F32, name="shared")
         for t in range(PACK):
-            plane = keep.tile([P, U], F32, name="skip_sb%d" % t)
-            nc.sync.dma_start(plane[:], skip_rows[:, t, :])
+            plane = shared[:, U // 2 :] if t == 2 else keep.tile([P, U], F32, name="skip_sb%d" % t)[:]
+            nc.sync.dma_start(plane, skip_rows[:, t, :])
             skip_sb.append(plane)
         w2_codes = keep.tile([P, N], I32, name="w2_codes", align_bytes=64)
         nc.sync.dma_start(w2_codes[:], w2_words[0].rearrange("p n r -> p (n r)").bitcast(I32))
@@ -66,105 +65,152 @@ def tile_picked_unet_none_e_kernel(
             nc.vector.memset(window[:], 0.0)
             up.append(window)
 
-        halves = [slice(a * HALF, (a + 1) * HALF) for a in range(2)]
-        list_halves = [slice(a * HALF // 16, (a + 1) * HALF // 16) for a in range(2)]
         x_bf = keep.tile([P, S, PACK], BF16, name="x_bf", align_bytes=64)
-        for j in range(PACK):
+        for j in range(PACK - 1):
             nc.vector.tensor_copy(x_bf[:, :, j], x_raw[j][:].indirect(offs_sb[:]))
+        for a in range(2):
+            nc.vector.tensor_copy(
+                x_bf[:, a * HALF : (a + 1) * HALF, PACK - 1],
+                x_raw[PACK - 1][:].indirect(offs_sb[:, a * HALF // 16 : (a + 1) * HALF // 16]),
+            )
         x_codes = keep.tile([P, S], U32, name="x_codes", align_bytes=64)
         x_sc = keep.tile([P, S], U8, name="x_sc", align_bytes=64)
-        nc.vector.quantize_mx(out=x_codes[:].bitcast(FP8X4), scales=x_sc[:], in_=x_bf[:].rearrange("p s j -> p (s j)"))
+        for a in range(2):
+            cols = slice(a * HALF, (a + 1) * HALF)
+            nc.vector.quantize_mx(
+                out=x_codes[:, cols].bitcast(FP8X4), scales=x_sc[:, cols], in_=x_bf[:, cols, :].rearrange("p s j -> p (s j)")
+            )
 
-        w1_bf = [keep.tile([P, 2 * P * PACK], BF16, name="w1_bf%d" % u, align_bytes=64) for u in range(2)]
-        w1_codes = [keep.tile([P, 2 * P], U32, name="w1_codes%d" % u, align_bytes=64) for u in range(2)]
-        w1_sc = [keep.tile([P, 2 * P], U8, name="w1_sc%d" % u, align_bytes=64) for u in range(2)]
-        for b in range(2):
-            for u in range(2):
-                nc.scalar.copy(
-                    w1_bf[u][:].rearrange("p (e b mm mi j) -> p b mm j mi e", e=2, b=2, mi=2, j=PACK)[:, b],
-                    w1_raw[b][:].rearrange("p j (mm mi u e) -> p u mm j mi e", mi=2, u=2, e=2)[:, u],
-                )
-        for u in range(2):
-            nc.vector.quantize_mx(out=w1_codes[u][:].bitcast(FP8X4), scales=w1_sc[u][:], in_=w1_bf[u][:])
+        w1_bf = keep.tile([P, H * PACK], BF16, name="w1_bf", align_bytes=64)
+        w1_codes = keep.tile([P, H], U32, name="w1_codes", align_bytes=64)
+        w1_sc = keep.tile([P, H], U8, name="w1_sc", align_bytes=64)
+        w1_dst = w1_bf[:].rearrange("p (u e mm mi j) -> p u mm j mi e", u=2, e=2, mi=2, j=PACK)
+        w1_src = w1_raw[:].rearrange("p j (mm mi u e) -> p u mm j mi e", mi=2, u=2, e=2)
+
+        def quantize_w1(t0, t1):
+            nc.vector.quantize_mx(
+                out=w1_codes[:, t0 * P : t1 * P].bitcast(FP8X4),
+                scales=w1_sc[:, t0 * P : t1 * P],
+                in_=w1_bf[:, t0 * P * PACK : t1 * P * PACK],
+            )
+
+        def round_w1(u):
+            nc.vector.tensor_copy(w1_dst[:, u, :W1_VECTOR_PAIRS], w1_src[:, u, :W1_VECTOR_PAIRS])
+            nc.scalar.copy(w1_dst[:, u, W1_VECTOR_PAIRS:], w1_src[:, u, W1_VECTOR_PAIRS:])
+
+        round_w1(0)
+        quantize_w1(0, 1)
+        quantize_w1(1, 2)
+        round_w1(1)
+        quantize_w1(2, 4)
 
         h = [keep.tile([P, S], F32, name="h%d" % t) for t in range(PACK)]
 
-        def first_layer(t, cols):
-            width = cols.stop - cols.start
+        def first_layer(t, start, widths):
             bank = psum.tile([P, BANK], F32, name="bank")
-            nc.tensor.matmul_mx(
-                out=bank[:, :width],
-                lhsT=w1_codes[t // 2][:, (t % 2) * P : (t % 2 + 1) * P].bitcast(FP8X4),
-                lhsT_scale=w1_sc[t // 2][:, (t % 2) * P : (t % 2 + 1) * P],
-                rhs=x_codes[:, cols].bitcast(FP8X4),
-                rhs_scale=x_sc[:, cols],
-                start=True,
-                stop=True,
-            )
-            nc.scalar.copy(h[t][:, cols], bank[:, :width])
+            done = 0
+            for width in widths:
+                cols = slice(start + done, start + done + width)
+                nc.tensor.matmul_mx(
+                    out=bank[:, done : done + width],
+                    lhsT=w1_codes[:, t * P : (t + 1) * P].bitcast(FP8X4),
+                    lhsT_scale=w1_sc[:, t * P : (t + 1) * P],
+                    rhs=x_codes[:, cols].bitcast(FP8X4),
+                    rhs_scale=x_sc[:, cols],
+                    start=True,
+                    stop=True,
+                )
+                done = done + width
+            nc.scalar.copy(h[t][:, start : start + done], bank[:, :done])
+            return t, start, start + done
 
-        for a in range(2):
-            for t in range(2):
-                first_layer(t, halves[a])
-        for t in range(2, PACK):
-            first_layer(t, slice(0, S))
+        pieces = [
+            first_layer(0, 0, (128,)),
+            first_layer(1, 0, (128,)),
+            first_layer(0, 128, (128, 256)),
+            first_layer(1, 128, (128, 256)),
+            first_layer(2, 0, (S,)),
+            first_layer(3, 0, (S,)),
+        ]
 
-        z_rows = keep.tile([P, 3, U], BF16, name="z_rows")
-        z_slot = (0, 2, 1, 2)
-        for a in range(2):
-            for t in range(2):
-                nc.vector.tensor_copy(up[t][:].indirect(cell_sb[:, list_halves[a]]), h[t][:, halves[a]])
-        nc.gpsimd.tensor_tensor(z_rows[:, z_slot[0], :], up[0][:], skip_sb[0][:], ADD)
+        def scatter(t, start, stop):
+            nc.vector.tensor_copy(up[t][:].indirect(cell_sb[:, start // 16 : stop // 16]), h[t][:, start:stop])
+
+        z01 = keep.tile([P, 2, U], BF16, name="z01")
+        z23 = shared[:, :U].bitcast(BF16).rearrange("p (e v) -> p e v", e=2)
+        for piece in pieces[:4]:
+            scatter(*piece)
+        nc.gpsimd.tensor_tensor(z01[:, 0, :], up[0][:], skip_sb[0], ADD)
         cell_halves = [slice(a * U // 2, (a + 1) * U // 2) for a in range(2)]
         for cols in cell_halves:
-            nc.gpsimd.tensor_tensor(z_rows[:, z_slot[1], cols], up[1][:, cols], skip_sb[1][:, cols], ADD)
-        nc.vector.tensor_copy(up[2][:].indirect(cell_sb[:]), h[2][:])
-        nc.gpsimd.tensor_tensor(z_rows[:, z_slot[2], :], up[2][:], skip_sb[2][:], ADD)
-        nc.vector.tensor_copy(up[3][:].indirect(cell_sb[:]), h[3][:])
+            nc.gpsimd.tensor_tensor(z01[:, 1, cols], up[1][:, cols], skip_sb[1][:, cols], ADD)
+        scatter(*pieces[4])
+        nc.gpsimd.tensor_tensor(z23[:, 0, :], up[2][:], skip_sb[2], ADD)
+        scatter(*pieces[5])
 
         starts = [sum(CELL_CHUNKS[:c]) for c in range(len(CELL_CHUNKS))]
         chunks = [slice(s, s + w) for s, w in zip(starts, CELL_CHUNKS)]
         z_bf = keep.tile([P, U, PACK], BF16, name="z_bf", align_bytes=64)
         for cols in cell_halves:
-            nc.scalar.copy(z_bf[:, cols, 0:2], z_rows[:, 0:3:2, cols].rearrange("p e v -> p v e"))
+            nc.scalar.copy(z_bf[:, cols, 0:2], z01[:, :, cols].rearrange("p e v -> p v e"))
 
         out_rows = out.rearrange("(g p) v -> p g v", p=P)
 
-        def add_last(c):
-            nc.vector.tensor_tensor(z_rows[:, z_slot[3], chunks[c]], up[3][:, chunks[c]], skip_sb[3][:, chunks[c]], ADD)
+        def add_last(first, last):
+            cols = slice(chunks[first].start, chunks[last].stop)
+            nc.vector.tensor_tensor(z23[:, 1, cols], up[3][:, cols], skip_sb[3][:, cols], ADD)
 
-        def weave(c):
-            move = nc.scalar.copy if c == 1 else nc.vector.tensor_copy
-            move(z_bf[:, chunks[c], 2:4], z_rows[:, 1:3, chunks[c]].rearrange("p e v -> p v e"))
+        def weave(c, move):
+            move(z_bf[:, chunks[c], 2:4], z23[:, :, chunks[c]].rearrange("p e v -> p v e"))
 
-        def second_layer(c):
+        def second_layer(c, banks):
             width = CELL_CHUNKS[c]
             z_codes = keep.tile([P, width], U32, name="z_codes%d" % c, align_bytes=64)
             z_sc = keep.tile([P, width], U8, name="z_sc%d" % c, align_bytes=64)
             nc.vector.quantize_mx(
                 out=z_codes[:].bitcast(FP8X4), scales=z_sc[:], in_=z_bf[:, chunks[c], :].rearrange("p v t -> p (v t)")
             )
-            bank = psum.tile([P, BANK], F32, name="bank")
-            for g in range(2):
-                nc.tensor.matmul_mx(
-                    out=bank[:, g * width : (g + 1) * width],
-                    lhsT=w2_codes[:, g * P : (g + 1) * P].bitcast(FP8X4),
-                    lhsT_scale=w2_sc[:, g * P : (g + 1) * P],
-                    rhs=z_codes[:].bitcast(FP8X4),
-                    rhs_scale=z_sc[:],
-                    start=True,
-                    stop=True,
-                )
-            res = keep.tile([P, 2, width], F32, name="res%d" % c)
-            move = nc.vector.tensor_copy if c == len(CELL_CHUNKS) - 1 else nc.scalar.copy
-            move(res[:].rearrange("p g v -> p (g v)"), bank[:, : 2 * width])
-            nc.sync.dma_start(out_rows[:, :, chunks[c]], res[:])
+            per_bank = 2 // banks
+            sums = []
+            for b in range(banks):
+                bank = psum.tile([P, BANK], F32, name="bank")
+                for i in range(per_bank):
+                    g = b * per_bank + i
+                    nc.tensor.matmul_mx(
+                        out=bank[:, i * width : (i + 1) * width],
+                        lhsT=w2_codes[:, g * P : (g + 1) * P].bitcast(FP8X4),
+                        lhsT_scale=w2_sc[:, g * P : (g + 1) * P],
+                        rhs=z_codes[:].bitcast(FP8X4),
+                        rhs_scale=z_sc[:],
+                        start=True,
+                        stop=True,
+                    )
+                sums.append(bank[:, : per_bank * width])
+            return sums
 
-        n = len(CELL_CHUNKS)
-        for step in range(n + 2):
-            if step < n:
-                add_last(step)
-            if 1 <= step <= n:
-                weave(step - 1)
-            if step >= 2:
-                second_layer(step - 2)
+        def store(c, sums, moves):
+            res = keep.tile([P, 2 * CELL_CHUNKS[c]], F32, name="res%d" % c)
+            share = 2 * CELL_CHUNKS[c] // len(sums)
+            for b, move in enumerate(moves):
+                move(res[:, b * share : (b + 1) * share], sums[b])
+            nc.sync.dma_start(out_rows[:, :, chunks[c]], res[:].rearrange("p (g v) -> p g v", g=2))
+
+        on_vector, on_scalar = nc.vector.tensor_copy, nc.scalar.copy
+        add_last(0, 0)
+        add_last(1, 2)
+        weave(0, on_vector)
+        weave(1, on_scalar)
+        weave(2, on_scalar)
+        add_last(3, 3)
+        store(0, second_layer(0, 1), [on_scalar])
+        weave(3, on_vector)
+        store(1, second_layer(1, 1), [on_scalar])
+        add_last(4, 5)
+        store(2, second_layer(2, 1), [on_scalar])
+        store(3, second_layer(3, 1), [on_scalar])
+        weave(4, on_vector)
+        weave(5, on_vector)
+        sums4 = second_layer(4, 1)
+        sums5 = second_layer(5, 2)
+        store(4, sums4, [on_vector])
+        store(5, sums5, [on_scalar, on_vector])

@@ -17,10 +17,14 @@ ADD = mybir.AluOpType.add
 P = 128
 PACK = 4
 BANK = 512
-HALF = S // 2
-CELL_CHUNKS = (128, 256, 128, 256, 128, 128)
+LIST_ROWS = 16
+QUADRANT = 32
+OUT_TILES = N // P
+
+FIRST_POINTS = 128
+REST_POINTS = (128, 256)
 W1_VECTOR_PAIRS = 40
-FIRST_PIECE = 128
+CELL_CHUNKS = (128, 256, 256, 128, 128, 128)
 
 
 def tile_picked_unet_none_e_kernel(
@@ -31,33 +35,35 @@ def tile_picked_unet_none_e_kernel(
         keep = ctx.enter_context(tc.tile_pool(name="keep", bufs=1))
         psum = ctx.enter_context(tc.psum_pool(name="psum", bufs=8))
 
-        offs_sb = keep.tile([P, S // 16], U16, name="offs_sb")
-        cell_sb = keep.tile([P, S // 16], U16, name="cell_sb")
-
+        offs_sb = keep.tile([P, S // LIST_ROWS], U16, name="offs_sb")
+        cell_sb = keep.tile([P, S // LIST_ROWS], U16, name="cell_sb")
         x_rows = xT.rearrange("(p j) t -> p j t", j=PACK)
-        x_raw = []
-        for j in range(PACK):
-            plane = keep.tile([P, T], F32, name="x_raw%d" % j)
-            nc.sync.dma_start(plane[:], x_rows[:, j, :])
-            x_raw.append(plane)
-            if j == 0:
-                nc.sync.dma_start(offs_sb[:], offs)
+        x_raw = [keep.tile([P, T], F32, name="x_raw%d" % j) for j in range(PACK)]
+        nc.sync.dma_start(x_raw[0][:], x_rows[:, 0, :])
+        nc.sync.dma_start(offs_sb[:], offs)
+        for j in range(1, PACK):
+            nc.sync.dma_start(x_raw[j][:], x_rows[:, j, :])
         w1_raw = keep.tile([P, PACK, H], F32, name="w1_raw")
         nc.sync.dma_start(w1_raw[:], w1.rearrange("(p j) c -> p j c", j=PACK))
         nc.sync.dma_start(cell_sb[:], cell)
+
+        z23_skip2 = keep.tile([P, U // 2 + U], F32, name="z23_skip2")
         skip_rows = skip.rearrange("(p t) v -> p t v", t=PACK)
         skip_sb = []
-        shared = keep.tile([P, U // 2 + U], F32, name="shared")
         for t in range(PACK):
-            plane = shared[:, U // 2 :] if t == 2 else keep.tile([P, U], F32, name="skip_sb%d" % t)[:]
+            plane = z23_skip2[:, U // 2 :] if t == 2 else keep.tile([P, U], F32, name="skip_sb%d" % t)[:]
             nc.sync.dma_start(plane, skip_rows[:, t, :])
             skip_sb.append(plane)
+
         w2_codes = keep.tile([P, N], I32, name="w2_codes", align_bytes=64)
         nc.sync.dma_start(w2_codes[:], w2_words[0].rearrange("p n r -> p (n r)").bitcast(I32))
         w2_sc = keep.tile([P, N], U8, name="w2_sc", align_bytes=64)
         nc.vector.memset(w2_sc[:].bitcast(I32), 0)
-        for q in range(4):
-            nc.sync.dma_start(w2_sc[32 * q : 32 * q + 4, :].bitcast(I32), w2_scales[0, 4 * q : 4 * q + 4, :].bitcast(I32))
+        for q in range(P // QUADRANT):
+            nc.sync.dma_start(
+                w2_sc[QUADRANT * q : QUADRANT * q + 4, :].bitcast(I32),
+                w2_scales[0, 4 * q : 4 * q + 4, :].bitcast(I32),
+            )
 
         up = []
         for t in range(PACK):
@@ -68,17 +74,20 @@ def tile_picked_unet_none_e_kernel(
         x_bf = keep.tile([P, S, PACK], BF16, name="x_bf", align_bytes=64)
         for j in range(PACK - 1):
             nc.vector.tensor_copy(x_bf[:, :, j], x_raw[j][:].indirect(offs_sb[:]))
+        half = S // 2
         for a in range(2):
             nc.vector.tensor_copy(
-                x_bf[:, a * HALF : (a + 1) * HALF, PACK - 1],
-                x_raw[PACK - 1][:].indirect(offs_sb[:, a * HALF // 16 : (a + 1) * HALF // 16]),
+                x_bf[:, a * half : (a + 1) * half, PACK - 1],
+                x_raw[PACK - 1][:].indirect(offs_sb[:, a * half // LIST_ROWS : (a + 1) * half // LIST_ROWS]),
             )
         x_codes = keep.tile([P, S], U32, name="x_codes", align_bytes=64)
         x_sc = keep.tile([P, S], U8, name="x_sc", align_bytes=64)
         for a in range(2):
-            cols = slice(a * HALF, (a + 1) * HALF)
+            points = slice(a * half, (a + 1) * half)
             nc.vector.quantize_mx(
-                out=x_codes[:, cols].bitcast(FP8X4), scales=x_sc[:, cols], in_=x_bf[:, cols, :].rearrange("p s j -> p (s j)")
+                out=x_codes[:, points].bitcast(FP8X4),
+                scales=x_sc[:, points],
+                in_=x_bf[:, points, :].rearrange("p s j -> p (s j)"),
             )
 
         w1_bf = keep.tile([P, H * PACK], BF16, name="w1_bf", align_bytes=64)
@@ -87,16 +96,16 @@ def tile_picked_unet_none_e_kernel(
         w1_dst = w1_bf[:].rearrange("p (u e mm mi j) -> p u mm j mi e", u=2, e=2, mi=2, j=PACK)
         w1_src = w1_raw[:].rearrange("p j (mm mi u e) -> p u mm j mi e", mi=2, u=2, e=2)
 
-        def quantize_w1(t0, t1):
-            nc.vector.quantize_mx(
-                out=w1_codes[:, t0 * P : t1 * P].bitcast(FP8X4),
-                scales=w1_sc[:, t0 * P : t1 * P],
-                in_=w1_bf[:, t0 * P * PACK : t1 * P * PACK],
-            )
-
         def round_w1(u):
             nc.vector.tensor_copy(w1_dst[:, u, :W1_VECTOR_PAIRS], w1_src[:, u, :W1_VECTOR_PAIRS])
             nc.scalar.copy(w1_dst[:, u, W1_VECTOR_PAIRS:], w1_src[:, u, W1_VECTOR_PAIRS:])
+
+        def quantize_w1(t_from, t_to):
+            nc.vector.quantize_mx(
+                out=w1_codes[:, t_from * P : t_to * P].bitcast(FP8X4),
+                scales=w1_sc[:, t_from * P : t_to * P],
+                in_=w1_bf[:, t_from * P * PACK : t_to * P * PACK],
+            )
 
         round_w1(0)
         quantize_w1(0, 1)
@@ -106,17 +115,17 @@ def tile_picked_unet_none_e_kernel(
 
         h = [keep.tile([P, S], F32, name="h%d" % t) for t in range(PACK)]
 
-        def first_layer(t, start, widths):
+        def first_product(t, start, widths):
             bank = psum.tile([P, BANK], F32, name="bank")
             done = 0
             for width in widths:
-                cols = slice(start + done, start + done + width)
+                points = slice(start + done, start + done + width)
                 nc.tensor.matmul_mx(
                     out=bank[:, done : done + width],
                     lhsT=w1_codes[:, t * P : (t + 1) * P].bitcast(FP8X4),
                     lhsT_scale=w1_sc[:, t * P : (t + 1) * P],
-                    rhs=x_codes[:, cols].bitcast(FP8X4),
-                    rhs_scale=x_sc[:, cols],
+                    rhs=x_codes[:, points].bitcast(FP8X4),
+                    rhs_scale=x_sc[:, points],
                     start=True,
                     stop=True,
                 )
@@ -124,60 +133,60 @@ def tile_picked_unet_none_e_kernel(
             nc.scalar.copy(h[t][:, start : start + done], bank[:, :done])
             return t, start, start + done
 
-        pieces = [
-            first_layer(0, 0, (128,)),
-            first_layer(1, 0, (128,)),
-            first_layer(0, 128, (128, 256)),
-            first_layer(1, 128, (128, 256)),
-            first_layer(2, 0, (S,)),
-            first_layer(3, 0, (S,)),
-        ]
+        early_pieces = [first_product(t, 0, (FIRST_POINTS,)) for t in range(2)]
+        early_pieces.extend([first_product(t, FIRST_POINTS, REST_POINTS) for t in range(2)])
+        piece2 = first_product(2, 0, (S,))
+        piece3 = first_product(3, 0, (S,))
 
         def scatter(t, start, stop):
-            nc.vector.tensor_copy(up[t][:].indirect(cell_sb[:, start // 16 : stop // 16]), h[t][:, start:stop])
+            entries = cell_sb[:, start // LIST_ROWS : stop // LIST_ROWS]
+            nc.vector.tensor_copy(up[t][:].indirect(entries), h[t][:, start:stop])
 
         z01 = keep.tile([P, 2, U], BF16, name="z01")
-        z23 = shared[:, :U].bitcast(BF16).rearrange("p (e v) -> p e v", e=2)
-        for piece in pieces[:4]:
+        z23 = z23_skip2[:, :U].bitcast(BF16).rearrange("p (e v) -> p e v", e=2)
+        for piece in early_pieces:
             scatter(*piece)
         nc.gpsimd.tensor_tensor(z01[:, 0, :], up[0][:], skip_sb[0], ADD)
         cell_halves = [slice(a * U // 2, (a + 1) * U // 2) for a in range(2)]
-        for cols in cell_halves:
-            nc.gpsimd.tensor_tensor(z01[:, 1, cols], up[1][:, cols], skip_sb[1][:, cols], ADD)
-        scatter(*pieces[4])
+        for cells in cell_halves:
+            nc.gpsimd.tensor_tensor(z01[:, 1, cells], up[1][:, cells], skip_sb[1][:, cells], ADD)
+        scatter(*piece2)
         nc.gpsimd.tensor_tensor(z23[:, 0, :], up[2][:], skip_sb[2], ADD)
-        scatter(*pieces[5])
+        scatter(*piece3)
+
+        z_bf = keep.tile([P, U, PACK], BF16, name="z_bf", align_bytes=64)
+        for cells in cell_halves:
+            nc.scalar.copy(z_bf[:, cells, 0:2], z01[:, :, cells].rearrange("p e v -> p v e"))
 
         starts = [sum(CELL_CHUNKS[:c]) for c in range(len(CELL_CHUNKS))]
-        chunks = [slice(s, s + w) for s, w in zip(starts, CELL_CHUNKS)]
-        z_bf = keep.tile([P, U, PACK], BF16, name="z_bf", align_bytes=64)
-        for cols in cell_halves:
-            nc.scalar.copy(z_bf[:, cols, 0:2], z01[:, :, cols].rearrange("p e v -> p v e"))
-
+        chunks = [slice(start, start + width) for start, width in zip(starts, CELL_CHUNKS)]
         out_rows = out.rearrange("(g p) v -> p g v", p=P)
+        res = keep.tile([P, OUT_TILES, U], F32, name="res")
 
-        def add_last(first, last):
-            cols = slice(chunks[first].start, chunks[last].stop)
-            nc.vector.tensor_tensor(z23[:, 1, cols], up[3][:, cols], skip_sb[3][:, cols], ADD)
+        def add_plane3(first, last):
+            cells = slice(chunks[first].start, chunks[last].stop)
+            nc.vector.tensor_tensor(z23[:, 1, cells], up[3][:, cells], skip_sb[3][:, cells], ADD)
 
-        def weave(c, move):
+        def weave23(c, move):
             move(z_bf[:, chunks[c], 2:4], z23[:, :, chunks[c]].rearrange("p e v -> p v e"))
 
-        def second_layer(c, banks):
+        def second_product(c, banks):
             width = CELL_CHUNKS[c]
             z_codes = keep.tile([P, width], U32, name="z_codes%d" % c, align_bytes=64)
             z_sc = keep.tile([P, width], U8, name="z_sc%d" % c, align_bytes=64)
             nc.vector.quantize_mx(
-                out=z_codes[:].bitcast(FP8X4), scales=z_sc[:], in_=z_bf[:, chunks[c], :].rearrange("p v t -> p (v t)")
+                out=z_codes[:].bitcast(FP8X4),
+                scales=z_sc[:],
+                in_=z_bf[:, chunks[c], :].rearrange("p v t -> p (v t)"),
             )
-            per_bank = 2 // banks
+            per_bank = OUT_TILES // banks
             sums = []
             for b in range(banks):
                 bank = psum.tile([P, BANK], F32, name="bank")
-                for i in range(per_bank):
-                    g = b * per_bank + i
+                for place in range(per_bank):
+                    g = b * per_bank + place
                     nc.tensor.matmul_mx(
-                        out=bank[:, i * width : (i + 1) * width],
+                        out=bank[:, place * width : (place + 1) * width],
                         lhsT=w2_codes[:, g * P : (g + 1) * P].bitcast(FP8X4),
                         lhsT_scale=w2_sc[:, g * P : (g + 1) * P],
                         rhs=z_codes[:].bitcast(FP8X4),
@@ -185,32 +194,32 @@ def tile_picked_unet_none_e_kernel(
                         start=True,
                         stop=True,
                     )
-                sums.append(bank[:, : per_bank * width])
+                sums.append(bank[:, : per_bank * width].rearrange("p (g v) -> p g v", g=per_bank))
             return sums
 
-        def store(c, sums, moves):
-            res = keep.tile([P, 2 * CELL_CHUNKS[c]], F32, name="res%d" % c)
-            share = 2 * CELL_CHUNKS[c] // len(sums)
-            for b, move in enumerate(moves):
-                move(res[:, b * share : (b + 1) * share], sums[b])
-            nc.sync.dma_start(out_rows[:, :, chunks[c]], res[:].rearrange("p (g v) -> p g v", g=2))
+        def store(c, sums, move):
+            per_bank = OUT_TILES // len(sums)
+            for b, bank_sums in enumerate(sums):
+                move(res[:, b * per_bank : (b + 1) * per_bank, chunks[c]], bank_sums)
+            nc.sync.dma_start(out_rows[:, :, chunks[c]], res[:, :, chunks[c]])
 
         on_vector, on_scalar = nc.vector.tensor_copy, nc.scalar.copy
-        add_last(0, 0)
-        add_last(1, 2)
-        weave(0, on_vector)
-        weave(1, on_scalar)
-        weave(2, on_scalar)
-        add_last(3, 3)
-        store(0, second_layer(0, 1), [on_scalar])
-        weave(3, on_vector)
-        store(1, second_layer(1, 1), [on_scalar])
-        add_last(4, 5)
-        store(2, second_layer(2, 1), [on_scalar])
-        store(3, second_layer(3, 1), [on_scalar])
-        weave(4, on_vector)
-        weave(5, on_vector)
-        sums4 = second_layer(4, 1)
-        sums5 = second_layer(5, 2)
-        store(4, sums4, [on_vector])
-        store(5, sums5, [on_scalar, on_vector])
+        add_plane3(0, 0)
+        weave23(0, on_scalar)
+        add_plane3(1, 1)
+        add_plane3(2, 3)
+        weave23(2, on_scalar)
+        weave23(3, on_scalar)
+        store(0, second_product(0, 1), on_scalar)
+        weave23(1, on_vector)
+        add_plane3(4, 5)
+        store(1, second_product(1, 2), on_scalar)
+        weave23(4, on_vector)
+        store(2, second_product(2, 2), on_scalar)
+        weave23(5, on_vector)
+        sums3 = second_product(3, 1)
+        sums4 = second_product(4, 1)
+        sums5 = second_product(5, 2)
+        store(3, sums3, on_vector)
+        store(4, sums4, on_scalar)
+        store(5, sums5, on_vector)

@@ -1,6 +1,7 @@
 from contextlib import ExitStack
 
 import concourse.mybir as mybir
+from concourse.masks import make_identity
 
 K, T, S, H, N, U = 512, 2048, 512, 512, 256, 1024
 FLOPS = 2 * K * H * S + 2 * H * N * U
@@ -23,8 +24,8 @@ OUT_TILES = N // P
 
 FIRST_POINTS = 128
 REST_POINTS = (128, 256)
-W1_VECTOR_PAIRS = 40
-CELL_CHUNKS = (128, 256, 256, 128, 128, 128)
+CHUNK = 256
+CHUNKS = U // CHUNK
 
 
 def tile_picked_unet_none_e_kernel(
@@ -33,7 +34,8 @@ def tile_picked_unet_none_e_kernel(
     nc = tc.nc
     with ExitStack() as ctx:
         keep = ctx.enter_context(tc.tile_pool(name="keep", bufs=1))
-        psum = ctx.enter_context(tc.psum_pool(name="psum", bufs=8))
+        held = ctx.enter_context(tc.psum_pool(name="held", bufs=1))
+        psum = ctx.enter_context(tc.psum_pool(name="psum", bufs=6))
 
         offs_sb = keep.tile([P, S // LIST_ROWS], U16, name="offs_sb")
         cell_sb = keep.tile([P, S // LIST_ROWS], U16, name="cell_sb")
@@ -43,17 +45,26 @@ def tile_picked_unet_none_e_kernel(
         nc.sync.dma_start(offs_sb[:], offs)
         for j in range(1, PACK):
             nc.sync.dma_start(x_raw[j][:], x_rows[:, j, :])
-        w1_raw = keep.tile([P, PACK, H], F32, name="w1_raw")
-        nc.sync.dma_start(w1_raw[:], w1.rearrange("(p j) c -> p j c", j=PACK))
+        w1_rows = w1.rearrange("(p j) c -> p j c", j=PACK)
+        w1_raw = []
+        for a in range(2):
+            columns = keep.tile([P, PACK, H // 2], F32, name="w1_raw%d" % a)
+            nc.sync.dma_start(columns[:], w1_rows[:, :, a * H // 2 : (a + 1) * H // 2])
+            w1_raw.append(columns)
         nc.sync.dma_start(cell_sb[:], cell)
 
-        z23_skip2 = keep.tile([P, U // 2 + U], F32, name="z23_skip2")
+        rest = U - CHUNK
         skip_rows = skip.rearrange("(p t) v -> p t v", t=PACK)
+        skip3_rest = keep.tile([P, rest], F32, name="skip3_rest")
+        nc.sync.dma_start(skip3_rest[:], skip_rows[:, 3, CHUNK:])
+        z23_skip2 = keep.tile([P, rest // 2 + U], F32, name="z23_skip2")
         skip_sb = []
-        for t in range(PACK):
-            plane = z23_skip2[:, U // 2 :] if t == 2 else keep.tile([P, U], F32, name="skip_sb%d" % t)[:]
+        for t in range(PACK - 1):
+            plane = z23_skip2[:, rest // 2 :] if t == 2 else keep.tile([P, U], F32, name="skip_sb%d" % t)[:]
             nc.sync.dma_start(plane, skip_rows[:, t, :])
             skip_sb.append(plane)
+        skip3_first = keep.tile([P, CHUNK], F32, name="skip3_first")
+        nc.sync.dma_start(skip3_first[:], skip_rows[:, 3, :CHUNK])
 
         w2_codes = keep.tile([P, N], I32, name="w2_codes", align_bytes=64)
         nc.sync.dma_start(w2_codes[:], w2_words[0].rearrange("p n r -> p (n r)").bitcast(I32))
@@ -94,11 +105,14 @@ def tile_picked_unet_none_e_kernel(
         w1_codes = keep.tile([P, H], U32, name="w1_codes", align_bytes=64)
         w1_sc = keep.tile([P, H], U8, name="w1_sc", align_bytes=64)
         w1_dst = w1_bf[:].rearrange("p (u e mm mi j) -> p u mm j mi e", u=2, e=2, mi=2, j=PACK)
-        w1_src = w1_raw[:].rearrange("p j (mm mi u e) -> p u mm j mi e", mi=2, u=2, e=2)
+        w1_src = [
+            columns[:].rearrange("p j (mm mi u e) -> p u mm j mi e", mi=2, u=2, e=2) for columns in w1_raw
+        ]
+        pairs = P // 4
 
         def round_w1(u):
-            nc.vector.tensor_copy(w1_dst[:, u, :W1_VECTOR_PAIRS], w1_src[:, u, :W1_VECTOR_PAIRS])
-            nc.scalar.copy(w1_dst[:, u, W1_VECTOR_PAIRS:], w1_src[:, u, W1_VECTOR_PAIRS:])
+            nc.scalar.copy(w1_dst[:, u, :pairs], w1_src[0][:, u])
+            nc.vector.tensor_copy(w1_dst[:, u, pairs:], w1_src[1][:, u])
 
         def quantize_w1(t_from, t_to):
             nc.vector.quantize_mx(
@@ -108,9 +122,9 @@ def tile_picked_unet_none_e_kernel(
             )
 
         round_w1(0)
+        round_w1(1)
         quantize_w1(0, 1)
         quantize_w1(1, 2)
-        round_w1(1)
         quantize_w1(2, 4)
 
         h = [keep.tile([P, S], F32, name="h%d" % t) for t in range(PACK)]
@@ -142,8 +156,32 @@ def tile_picked_unet_none_e_kernel(
             entries = cell_sb[:, start // LIST_ROWS : stop // LIST_ROWS]
             nc.vector.tensor_copy(up[t][:].indirect(entries), h[t][:, start:stop])
 
+        chunks = [slice(c * CHUNK, (c + 1) * CHUNK) for c in range(CHUNKS)]
+        ident = keep.tile([P, P], F32, name="ident")
+        make_identity(nc, ident[:])
+        skip3_turned = keep.tile([P, rest], F32, name="skip3_turned")
+        skip3_psum = {}
+        for b, group in enumerate(((1,), (2, 3))):
+            width = CHUNK * len(group)
+            first = chunks[group[0]].start - CHUNK
+            turned = skip3_turned[:, first : first + width]
+            bank = psum.tile([P, BANK], F32, name="bank")
+            for block in range(0, width, P):
+                nc.tensor.transpose(
+                    bank[:, block : block + P], skip3_rest[:, first + block : first + block + P], ident[:]
+                )
+            nc.scalar.copy(turned, bank[:, :width])
+            back = held.tile([P, BANK], F32, name="skip3_bank%d" % b)
+            for block in range(0, width, P):
+                nc.tensor.transpose(back[:, block : block + P], turned[:, block : block + P], ident[:])
+            for place, c in enumerate(group):
+                skip3_psum[c] = back[:, place * CHUNK : (place + 1) * CHUNK]
+
+        z_bf = keep.tile([P, U, PACK], BF16, name="z_bf", align_bytes=64)
         z01 = keep.tile([P, 2, U], BF16, name="z01")
-        z23 = z23_skip2[:, :U].bitcast(BF16).rearrange("p (e v) -> p e v", e=2)
+        pitch = rest + 2 * CHUNK
+        z23 = z23_skip2[:, :pitch].bitcast(BF16).rearrange("p (e v) -> p e v", e=2)
+        inner = [slice((c - 1) * CHUNK, c * CHUNK) for c in range(CHUNKS)]
         for piece in early_pieces:
             scatter(*piece)
         nc.gpsimd.tensor_tensor(z01[:, 0, :], up[0][:], skip_sb[0], ADD)
@@ -151,75 +189,56 @@ def tile_picked_unet_none_e_kernel(
         for cells in cell_halves:
             nc.gpsimd.tensor_tensor(z01[:, 1, cells], up[1][:, cells], skip_sb[1][:, cells], ADD)
         scatter(*piece2)
-        nc.gpsimd.tensor_tensor(z23[:, 0, :], up[2][:], skip_sb[2], ADD)
+        nc.gpsimd.tensor_tensor(z_bf[:, chunks[0], 2], up[2][:, chunks[0]], skip_sb[2][:, chunks[0]], ADD)
+        nc.gpsimd.tensor_tensor(z23[:, 0, :rest], up[2][:, CHUNK:], skip_sb[2][:, CHUNK:], ADD)
         scatter(*piece3)
-
-        z_bf = keep.tile([P, U, PACK], BF16, name="z_bf", align_bytes=64)
         for cells in cell_halves:
             nc.scalar.copy(z_bf[:, cells, 0:2], z01[:, :, cells].rearrange("p e v -> p v e"))
 
-        starts = [sum(CELL_CHUNKS[:c]) for c in range(len(CELL_CHUNKS))]
-        chunks = [slice(start, start + width) for start, width in zip(starts, CELL_CHUNKS)]
         out_rows = out.rearrange("(g p) v -> p g v", p=P)
         res = keep.tile([P, OUT_TILES, U], F32, name="res")
-
-        def add_plane3(first, last):
-            cells = slice(chunks[first].start, chunks[last].stop)
-            nc.vector.tensor_tensor(z23[:, 1, cells], up[3][:, cells], skip_sb[3][:, cells], ADD)
+        on_vector, on_scalar = nc.vector.tensor_copy, nc.scalar.copy
 
         def weave23(c, move):
-            move(z_bf[:, chunks[c], 2:4], z23[:, :, chunks[c]].rearrange("p e v -> p v e"))
+            move(z_bf[:, chunks[c], 2:4], z23[:, :, inner[c]].rearrange("p e v -> p v e"))
 
-        def second_product(c, banks):
-            width = CELL_CHUNKS[c]
-            z_codes = keep.tile([P, width], U32, name="z_codes%d" % c, align_bytes=64)
-            z_sc = keep.tile([P, width], U8, name="z_sc%d" % c, align_bytes=64)
+        def second_product(c):
+            z_codes = keep.tile([P, CHUNK], U32, name="z_codes%d" % c, align_bytes=64)
+            z_sc = keep.tile([P, CHUNK], U8, name="z_sc%d" % c, align_bytes=64)
             nc.vector.quantize_mx(
                 out=z_codes[:].bitcast(FP8X4),
                 scales=z_sc[:],
                 in_=z_bf[:, chunks[c], :].rearrange("p v t -> p (v t)"),
             )
-            per_bank = OUT_TILES // banks
             sums = []
-            for b in range(banks):
+            for g in range(OUT_TILES):
                 bank = psum.tile([P, BANK], F32, name="bank")
-                for place in range(per_bank):
-                    g = b * per_bank + place
-                    nc.tensor.matmul_mx(
-                        out=bank[:, place * width : (place + 1) * width],
-                        lhsT=w2_codes[:, g * P : (g + 1) * P].bitcast(FP8X4),
-                        lhsT_scale=w2_sc[:, g * P : (g + 1) * P],
-                        rhs=z_codes[:].bitcast(FP8X4),
-                        rhs_scale=z_sc[:],
-                        start=True,
-                        stop=True,
-                    )
-                sums.append(bank[:, : per_bank * width].rearrange("p (g v) -> p g v", g=per_bank))
+                nc.tensor.matmul_mx(
+                    out=bank[:, :CHUNK],
+                    lhsT=w2_codes[:, g * P : (g + 1) * P].bitcast(FP8X4),
+                    lhsT_scale=w2_sc[:, g * P : (g + 1) * P],
+                    rhs=z_codes[:].bitcast(FP8X4),
+                    rhs_scale=z_sc[:],
+                    start=True,
+                    stop=True,
+                )
+                sums.append(bank[:, :CHUNK])
             return sums
 
-        def store(c, sums, move):
-            per_bank = OUT_TILES // len(sums)
-            for b, bank_sums in enumerate(sums):
-                move(res[:, b * per_bank : (b + 1) * per_bank, chunks[c]], bank_sums)
-            nc.sync.dma_start(out_rows[:, :, chunks[c]], res[:, :, chunks[c]])
+        def store(c, g, sums, move):
+            move(res[:, g, chunks[c]], sums[g])
+            nc.sync.dma_start(out_rows[:, g, chunks[c]], res[:, g, chunks[c]])
 
-        on_vector, on_scalar = nc.vector.tensor_copy, nc.scalar.copy
-        add_plane3(0, 0)
-        weave23(0, on_scalar)
-        add_plane3(1, 1)
-        add_plane3(2, 3)
-        weave23(2, on_scalar)
+        nc.gpsimd.tensor_tensor(z_bf[:, chunks[0], 3], up[3][:, chunks[0]], skip3_first[:], ADD)
+        for c in range(1, CHUNKS):
+            nc.vector.tensor_tensor(z23[:, 1, inner[c]], up[3][:, chunks[c]], skip3_psum[c], ADD)
+        weave23(1, on_scalar)
         weave23(3, on_scalar)
-        store(0, second_product(0, 1), on_scalar)
-        weave23(1, on_vector)
-        add_plane3(4, 5)
-        store(1, second_product(1, 2), on_scalar)
-        weave23(4, on_vector)
-        store(2, second_product(2, 2), on_scalar)
-        weave23(5, on_vector)
-        sums3 = second_product(3, 1)
-        sums4 = second_product(4, 1)
-        sums5 = second_product(5, 2)
-        store(3, sums3, on_vector)
-        store(4, sums4, on_scalar)
-        store(5, sums5, on_vector)
+        weave23(2, on_vector)
+        order = (0, 2, 1, 3)
+        sums = {c: second_product(c) for c in order}
+        store(0, 0, sums[0], on_scalar)
+        store(0, 1, sums[0], on_scalar)
+        for c in order[1:]:
+            store(c, 0, sums[c], on_scalar)
+            store(c, 1, sums[c], on_vector)

@@ -24,6 +24,7 @@ OUT_TILES = N // P
 
 FIRST_POINTS = 128
 REST_POINTS = (128, 256)
+W1_VECTOR_PAIRS = 40
 CHUNK = 256
 CHUNKS = U // CHUNK
 
@@ -45,12 +46,8 @@ def tile_picked_unet_none_e_kernel(
         nc.sync.dma_start(offs_sb[:], offs)
         for j in range(1, PACK):
             nc.sync.dma_start(x_raw[j][:], x_rows[:, j, :])
-        w1_rows = w1.rearrange("(p j) c -> p j c", j=PACK)
-        w1_raw = []
-        for a in range(2):
-            columns = keep.tile([P, PACK, H // 2], F32, name="w1_raw%d" % a)
-            nc.sync.dma_start(columns[:], w1_rows[:, :, a * H // 2 : (a + 1) * H // 2])
-            w1_raw.append(columns)
+        w1_raw = keep.tile([P, PACK, H], F32, name="w1_raw")
+        nc.sync.dma_start(w1_raw[:], w1.rearrange("(p j) c -> p j c", j=PACK))
         nc.sync.dma_start(cell_sb[:], cell)
 
         rest = U - CHUNK
@@ -105,14 +102,11 @@ def tile_picked_unet_none_e_kernel(
         w1_codes = keep.tile([P, H], U32, name="w1_codes", align_bytes=64)
         w1_sc = keep.tile([P, H], U8, name="w1_sc", align_bytes=64)
         w1_dst = w1_bf[:].rearrange("p (u e mm mi j) -> p u mm j mi e", u=2, e=2, mi=2, j=PACK)
-        w1_src = [
-            columns[:].rearrange("p j (mm mi u e) -> p u mm j mi e", mi=2, u=2, e=2) for columns in w1_raw
-        ]
-        pairs = P // 4
+        w1_src = w1_raw[:].rearrange("p j (mm mi u e) -> p u mm j mi e", mi=2, u=2, e=2)
 
         def round_w1(u):
-            nc.scalar.copy(w1_dst[:, u, :pairs], w1_src[0][:, u])
-            nc.vector.tensor_copy(w1_dst[:, u, pairs:], w1_src[1][:, u])
+            nc.vector.tensor_copy(w1_dst[:, u, :W1_VECTOR_PAIRS], w1_src[:, u, :W1_VECTOR_PAIRS])
+            nc.scalar.copy(w1_dst[:, u, W1_VECTOR_PAIRS:], w1_src[:, u, W1_VECTOR_PAIRS:])
 
         def quantize_w1(t_from, t_to):
             nc.vector.quantize_mx(
@@ -122,9 +116,9 @@ def tile_picked_unet_none_e_kernel(
             )
 
         round_w1(0)
-        round_w1(1)
         quantize_w1(0, 1)
         quantize_w1(1, 2)
+        round_w1(1)
         quantize_w1(2, 4)
 
         h = [keep.tile([P, S], F32, name="h%d" % t) for t in range(PACK)]

@@ -25,8 +25,11 @@ OUT_TILES = N // P
 FIRST_POINTS = 128
 REST_POINTS = (128, 256)
 W1_VECTOR_PAIRS = 40
-CHUNK = 256
-CHUNKS = U // CHUNK
+CELL_CHUNKS = (128, 256, 256, 128, 128, 128)
+FIRST_CELLS = CELL_CHUNKS[0]
+REST_CELLS = U - FIRST_CELLS
+ADD_GROUPS = ((1, 1), (2, 3), (4, 5))
+RING_BANKS = 8 - len(ADD_GROUPS)
 
 
 def tile_picked_unet_none_e_kernel(
@@ -36,7 +39,7 @@ def tile_picked_unet_none_e_kernel(
     with ExitStack() as ctx:
         keep = ctx.enter_context(tc.tile_pool(name="keep", bufs=1))
         held = ctx.enter_context(tc.psum_pool(name="held", bufs=1))
-        psum = ctx.enter_context(tc.psum_pool(name="psum", bufs=6))
+        psum = ctx.enter_context(tc.psum_pool(name="psum", bufs=RING_BANKS))
 
         offs_sb = keep.tile([P, S // LIST_ROWS], U16, name="offs_sb")
         cell_sb = keep.tile([P, S // LIST_ROWS], U16, name="cell_sb")
@@ -50,18 +53,20 @@ def tile_picked_unet_none_e_kernel(
         nc.sync.dma_start(w1_raw[:], w1.rearrange("(p j) c -> p j c", j=PACK))
         nc.sync.dma_start(cell_sb[:], cell)
 
-        rest = U - CHUNK
         skip_rows = skip.rearrange("(p t) v -> p t v", t=PACK)
-        skip3_rest = keep.tile([P, rest], F32, name="skip3_rest")
-        nc.sync.dma_start(skip3_rest[:], skip_rows[:, 3, CHUNK:])
-        z23_skip2 = keep.tile([P, rest // 2 + U], F32, name="z23_skip2")
+        skip3_rest = keep.tile([P, REST_CELLS], F32, name="skip3_rest")
+        nc.sync.dma_start(skip3_rest[:], skip_rows[:, 3, FIRST_CELLS:])
+        z23_skip2 = keep.tile([P, REST_CELLS // 2 + U], F32, name="z23_skip2")
         skip_sb = []
         for t in range(PACK - 1):
-            plane = z23_skip2[:, rest // 2 :] if t == 2 else keep.tile([P, U], F32, name="skip_sb%d" % t)[:]
+            if t == 2:
+                plane = z23_skip2[:, REST_CELLS // 2 :]
+            else:
+                plane = keep.tile([P, U], F32, name="skip_sb%d" % t)[:]
             nc.sync.dma_start(plane, skip_rows[:, t, :])
             skip_sb.append(plane)
-        skip3_first = keep.tile([P, CHUNK], F32, name="skip3_first")
-        nc.sync.dma_start(skip3_first[:], skip_rows[:, 3, :CHUNK])
+        skip3_first = keep.tile([P, FIRST_CELLS], F32, name="skip3_first")
+        nc.sync.dma_start(skip3_first[:], skip_rows[:, 3, :FIRST_CELLS])
 
         w2_codes = keep.tile([P, N], I32, name="w2_codes", align_bytes=64)
         nc.sync.dma_start(w2_codes[:], w2_words[0].rearrange("p n r -> p (n r)").bitcast(I32))
@@ -150,14 +155,15 @@ def tile_picked_unet_none_e_kernel(
             entries = cell_sb[:, start // LIST_ROWS : stop // LIST_ROWS]
             nc.vector.tensor_copy(up[t][:].indirect(entries), h[t][:, start:stop])
 
-        chunks = [slice(c * CHUNK, (c + 1) * CHUNK) for c in range(CHUNKS)]
+        starts = [sum(CELL_CHUNKS[:c]) for c in range(len(CELL_CHUNKS))]
+        chunks = [slice(start, start + width) for start, width in zip(starts, CELL_CHUNKS)]
         ident = keep.tile([P, P], F32, name="ident")
         make_identity(nc, ident[:])
-        skip3_turned = keep.tile([P, rest], F32, name="skip3_turned")
-        skip3_psum = {}
-        for b, group in enumerate(((1,), (2, 3))):
-            width = CHUNK * len(group)
-            first = chunks[group[0]].start - CHUNK
+        skip3_turned = keep.tile([P, REST_CELLS], F32, name="skip3_turned")
+        skip3_banks = []
+        for b, (first_chunk, last_chunk) in enumerate(ADD_GROUPS):
+            first = chunks[first_chunk].start - FIRST_CELLS
+            width = chunks[last_chunk].stop - chunks[first_chunk].start
             turned = skip3_turned[:, first : first + width]
             bank = psum.tile([P, BANK], F32, name="bank")
             for block in range(0, width, P):
@@ -165,17 +171,14 @@ def tile_picked_unet_none_e_kernel(
                     bank[:, block : block + P], skip3_rest[:, first + block : first + block + P], ident[:]
                 )
             nc.scalar.copy(turned, bank[:, :width])
-            back = held.tile([P, BANK], F32, name="skip3_bank%d" % b)
+            back = held.tile([P, BANK], F32, name="held%d" % b)
             for block in range(0, width, P):
                 nc.tensor.transpose(back[:, block : block + P], turned[:, block : block + P], ident[:])
-            for place, c in enumerate(group):
-                skip3_psum[c] = back[:, place * CHUNK : (place + 1) * CHUNK]
+            skip3_banks.append(back)
 
         z_bf = keep.tile([P, U, PACK], BF16, name="z_bf", align_bytes=64)
         z01 = keep.tile([P, 2, U], BF16, name="z01")
-        pitch = rest + 2 * CHUNK
-        z23 = z23_skip2[:, :pitch].bitcast(BF16).rearrange("p (e v) -> p e v", e=2)
-        inner = [slice((c - 1) * CHUNK, c * CHUNK) for c in range(CHUNKS)]
+        z23 = z23_skip2[:, : REST_CELLS + 2 * FIRST_CELLS].bitcast(BF16).rearrange("p (e v) -> p e v", e=2)
         for piece in early_pieces:
             scatter(*piece)
         nc.gpsimd.tensor_tensor(z01[:, 0, :], up[0][:], skip_sb[0], ADD)
@@ -183,8 +186,8 @@ def tile_picked_unet_none_e_kernel(
         for cells in cell_halves:
             nc.gpsimd.tensor_tensor(z01[:, 1, cells], up[1][:, cells], skip_sb[1][:, cells], ADD)
         scatter(*piece2)
-        nc.gpsimd.tensor_tensor(z_bf[:, chunks[0], 2], up[2][:, chunks[0]], skip_sb[2][:, chunks[0]], ADD)
-        nc.gpsimd.tensor_tensor(z23[:, 0, :rest], up[2][:, CHUNK:], skip_sb[2][:, CHUNK:], ADD)
+        nc.gpsimd.tensor_tensor(z_bf[:, :FIRST_CELLS, 2], up[2][:, :FIRST_CELLS], skip_sb[2][:, :FIRST_CELLS], ADD)
+        nc.gpsimd.tensor_tensor(z23[:, 0, :REST_CELLS], up[2][:, FIRST_CELLS:], skip_sb[2][:, FIRST_CELLS:], ADD)
         scatter(*piece3)
         for cells in cell_halves:
             nc.scalar.copy(z_bf[:, cells, 0:2], z01[:, :, cells].rearrange("p e v -> p v e"))
@@ -193,46 +196,83 @@ def tile_picked_unet_none_e_kernel(
         res = keep.tile([P, OUT_TILES, U], F32, name="res")
         on_vector, on_scalar = nc.vector.tensor_copy, nc.scalar.copy
 
-        def weave23(c, move):
-            move(z_bf[:, chunks[c], 2:4], z23[:, :, inner[c]].rearrange("p e v -> p v e"))
+        def add_plane3(b):
+            first, last = ADD_GROUPS[b]
+            start, stop = chunks[first].start - FIRST_CELLS, chunks[last].stop - FIRST_CELLS
+            nc.vector.tensor_tensor(
+                z23[:, 1, start:stop],
+                up[3][:, start + FIRST_CELLS : stop + FIRST_CELLS],
+                skip3_banks[b][:, : stop - start],
+                ADD,
+            )
 
-        def second_product(c):
-            z_codes = keep.tile([P, CHUNK], U32, name="z_codes%d" % c, align_bytes=64)
-            z_sc = keep.tile([P, CHUNK], U8, name="z_sc%d" % c, align_bytes=64)
+        def weave23(c, move):
+            inner = slice(chunks[c].start - FIRST_CELLS, chunks[c].stop - FIRST_CELLS)
+            move(z_bf[:, chunks[c], 2:4], z23[:, :, inner].rearrange("p e v -> p v e"))
+
+        def second_product(c, banks):
+            width = CELL_CHUNKS[c]
+            z_codes = keep.tile([P, width], U32, name="z_codes%d" % c, align_bytes=64)
+            z_sc = keep.tile([P, width], U8, name="z_sc%d" % c, align_bytes=64)
             nc.vector.quantize_mx(
                 out=z_codes[:].bitcast(FP8X4),
                 scales=z_sc[:],
                 in_=z_bf[:, chunks[c], :].rearrange("p v t -> p (v t)"),
             )
+            per_bank = OUT_TILES // banks
             sums = []
-            for g in range(OUT_TILES):
-                bank = psum.tile([P, BANK], F32, name="bank")
-                nc.tensor.matmul_mx(
-                    out=bank[:, :CHUNK],
-                    lhsT=w2_codes[:, g * P : (g + 1) * P].bitcast(FP8X4),
-                    lhsT_scale=w2_sc[:, g * P : (g + 1) * P],
-                    rhs=z_codes[:].bitcast(FP8X4),
-                    rhs_scale=z_sc[:],
-                    start=True,
-                    stop=True,
-                )
-                sums.append(bank[:, :CHUNK])
+            for b in range(banks):
+                if c >= len(CELL_CHUNKS) - len(ADD_GROUPS) and b == 0:
+                    bank = held.tile([P, BANK], F32, name="held%d" % ((c + 1) % len(ADD_GROUPS)))
+                else:
+                    bank = psum.tile([P, BANK], F32, name="bank")
+                for place in range(per_bank):
+                    g = b * per_bank + place
+                    nc.tensor.matmul_mx(
+                        out=bank[:, place * width : (place + 1) * width],
+                        lhsT=w2_codes[:, g * P : (g + 1) * P].bitcast(FP8X4),
+                        lhsT_scale=w2_sc[:, g * P : (g + 1) * P],
+                        rhs=z_codes[:].bitcast(FP8X4),
+                        rhs_scale=z_sc[:],
+                        start=True,
+                        stop=True,
+                    )
+                sums.append(bank[:, : per_bank * width].rearrange("p (g v) -> p g v", g=per_bank))
             return sums
 
-        def store(c, g, sums, move):
-            move(res[:, g, chunks[c]], sums[g])
-            nc.sync.dma_start(out_rows[:, g, chunks[c]], res[:, g, chunks[c]])
+        def unload(c, sums, *moves):
+            per_bank = OUT_TILES // len(sums)
+            for b, (bank_sums, move) in enumerate(zip(sums, moves)):
+                move(res[:, b * per_bank : (b + 1) * per_bank, chunks[c]], bank_sums)
 
-        nc.gpsimd.tensor_tensor(z_bf[:, chunks[0], 3], up[3][:, chunks[0]], skip3_first[:], ADD)
-        for c in range(1, CHUNKS):
-            nc.vector.tensor_tensor(z23[:, 1, inner[c]], up[3][:, chunks[c]], skip3_psum[c], ADD)
-        weave23(1, on_scalar)
+        def store(first, last, tiles):
+            cells = slice(chunks[first].start, chunks[last].stop)
+            nc.sync.dma_start(out_rows[:, tiles, cells], res[:, tiles, cells])
+
+        def store_by_tile(first, last):
+            for g in range(OUT_TILES):
+                store(first, last, slice(g, g + 1))
+
+        nc.gpsimd.tensor_tensor(z_bf[:, :FIRST_CELLS, 3], up[3][:, :FIRST_CELLS], skip3_first[:], ADD)
+        add_plane3(0)
+        add_plane3(1)
+        weave23(1, on_vector)
+        weave23(2, on_scalar)
         weave23(3, on_scalar)
-        weave23(2, on_vector)
-        order = (0, 2, 1, 3)
-        sums = {c: second_product(c) for c in order}
-        store(0, 0, sums[0], on_scalar)
-        store(0, 1, sums[0], on_scalar)
-        for c in order[1:]:
-            store(c, 0, sums[c], on_scalar)
-            store(c, 1, sums[c], on_vector)
+        unload(0, second_product(0, 1), on_scalar)
+        store(0, 0, slice(0, OUT_TILES))
+        unload(1, second_product(1, 2), on_scalar, on_scalar)
+        store_by_tile(1, 1)
+        add_plane3(2)
+        sums2 = second_product(2, 2)
+        weave23(4, on_vector)
+        weave23(5, on_vector)
+        sums3 = second_product(3, 1)
+        sums4 = second_product(4, 1)
+        sums5 = second_product(5, 2)
+        unload(2, sums2, on_scalar, on_vector)
+        store_by_tile(2, 2)
+        unload(3, sums3, on_scalar)
+        unload(4, sums4, on_vector)
+        unload(5, sums5, on_scalar, on_vector)
+        store_by_tile(3, 5)

@@ -1,7 +1,6 @@
 from contextlib import ExitStack
 
 import concourse.mybir as mybir
-from concourse.masks import make_identity
 
 K, T, S, H, N, U = 512, 2048, 512, 512, 256, 1024
 FLOPS = 2 * K * H * S + 2 * H * N * U
@@ -14,10 +13,12 @@ U16 = mybir.dt.uint16
 U8 = mybir.dt.uint8
 FP8X4 = mybir.dt.float8_e4m3fn_x4
 ADD = mybir.AluOpType.add
+COPY = mybir.ActivationFunctionType.Copy
 
 P = 128
 PACK = 4
 BANK = 512
+BANKS = 8
 LIST_ROWS = 16
 QUADRANT = 32
 OUT_TILES = N // P
@@ -25,11 +26,8 @@ OUT_TILES = N // P
 FIRST_POINTS = 128
 REST_POINTS = (128, 256)
 W1_VECTOR_PAIRS = 40
+PLANE3_VECTOR_POINTS = 128
 CELL_CHUNKS = (128, 256, 256, 128, 128, 128)
-FIRST_CELLS = CELL_CHUNKS[0]
-REST_CELLS = U - FIRST_CELLS
-ADD_GROUPS = ((1, 1), (2, 3), (4, 5))
-RING_BANKS = 8 - len(ADD_GROUPS)
 
 
 def tile_picked_unet_none_e_kernel(
@@ -38,8 +36,7 @@ def tile_picked_unet_none_e_kernel(
     nc = tc.nc
     with ExitStack() as ctx:
         keep = ctx.enter_context(tc.tile_pool(name="keep", bufs=1))
-        held = ctx.enter_context(tc.psum_pool(name="held", bufs=1))
-        psum = ctx.enter_context(tc.psum_pool(name="psum", bufs=RING_BANKS))
+        psum = ctx.enter_context(tc.psum_pool(name="psum", bufs=BANKS))
 
         offs_sb = keep.tile([P, S // LIST_ROWS], U16, name="offs_sb")
         cell_sb = keep.tile([P, S // LIST_ROWS], U16, name="cell_sb")
@@ -54,19 +51,15 @@ def tile_picked_unet_none_e_kernel(
         nc.sync.dma_start(cell_sb[:], cell)
 
         skip_rows = skip.rearrange("(p t) v -> p t v", t=PACK)
-        skip3_rest = keep.tile([P, REST_CELLS], F32, name="skip3_rest")
-        nc.sync.dma_start(skip3_rest[:], skip_rows[:, 3, FIRST_CELLS:])
-        z23_skip2 = keep.tile([P, REST_CELLS // 2 + U], F32, name="z23_skip2")
+        pair_words = keep.tile([P, 2 * U], F32, name="pair_words")
         skip_sb = []
-        for t in range(PACK - 1):
-            if t == 2:
-                plane = z23_skip2[:, REST_CELLS // 2 :]
+        for t in range(PACK):
+            if t == 1:
+                plane = pair_words[:, U:]
             else:
                 plane = keep.tile([P, U], F32, name="skip_sb%d" % t)[:]
             nc.sync.dma_start(plane, skip_rows[:, t, :])
             skip_sb.append(plane)
-        skip3_first = keep.tile([P, FIRST_CELLS], F32, name="skip3_first")
-        nc.sync.dma_start(skip3_first[:], skip_rows[:, 3, :FIRST_CELLS])
 
         w2_codes = keep.tile([P, N], I32, name="w2_codes", align_bytes=64)
         nc.sync.dma_start(w2_codes[:], w2_words[0].rearrange("p n r -> p (n r)").bitcast(I32))
@@ -108,10 +101,12 @@ def tile_picked_unet_none_e_kernel(
         w1_sc = keep.tile([P, H], U8, name="w1_sc", align_bytes=64)
         w1_dst = w1_bf[:].rearrange("p (u e mm mi j) -> p u mm j mi e", u=2, e=2, mi=2, j=PACK)
         w1_src = w1_raw[:].rearrange("p j (mm mi u e) -> p u mm j mi e", mi=2, u=2, e=2)
+        w1_dst3 = w1_bf[:].rearrange("p (u e m j) -> p u m j e", u=2, e=2, j=PACK)
+        w1_src3 = w1_raw[:].rearrange("p j (m u e) -> p u m j e", u=2, e=2)
 
         def round_w1(u):
             nc.vector.tensor_copy(w1_dst[:, u, :W1_VECTOR_PAIRS], w1_src[:, u, :W1_VECTOR_PAIRS])
-            nc.scalar.copy(w1_dst[:, u, W1_VECTOR_PAIRS:], w1_src[:, u, W1_VECTOR_PAIRS:])
+            nc.scalar.activation(w1_dst3[:, u, 2 * W1_VECTOR_PAIRS :], w1_src3[:, u, 2 * W1_VECTOR_PAIRS :], COPY)
 
         def quantize_w1(t_from, t_to):
             nc.vector.quantize_mx(
@@ -144,88 +139,56 @@ def tile_picked_unet_none_e_kernel(
                 )
                 done = done + width
             nc.scalar.copy(h[t][:, start : start + done], bank[:, :done])
-            return t, start, start + done
 
-        early_pieces = [first_product(t, 0, (FIRST_POINTS,)) for t in range(2)]
-        early_pieces.extend([first_product(t, FIRST_POINTS, REST_POINTS) for t in range(2)])
-        piece2 = first_product(2, 0, (S,))
-        piece3 = first_product(3, 0, (S,))
-
-        def scatter(t, start, stop):
+        def scatter_on_vector(t, start, stop):
             entries = cell_sb[:, start // LIST_ROWS : stop // LIST_ROWS]
             nc.vector.tensor_copy(up[t][:].indirect(entries), h[t][:, start:stop])
 
+        def scatter_on_scalar(t, start, stop):
+            entries = cell_sb[:, start // LIST_ROWS : stop // LIST_ROWS]
+            nc.scalar.activation(up[t][:].indirect(entries), h[t][:, start:stop], COPY)
+
+        pairs = pair_words[:].bitcast(BF16).rearrange("p (u v e) -> p u v e", u=2, e=2)
+
+        first_product(0, 0, (FIRST_POINTS,))
+        scatter_on_vector(0, 0, FIRST_POINTS)
+        first_product(0, FIRST_POINTS, REST_POINTS)
+        scatter_on_vector(0, FIRST_POINTS, S)
+        nc.gpsimd.tensor_tensor(pairs[:, 0, :, 0], up[0][:], skip_sb[0], ADD)
+        first_product(1, 0, (S,))
+        first_product(3, 0, (S,))
+        scatter_on_vector(3, 0, PLANE3_VECTOR_POINTS)
+        scatter_on_scalar(1, 0, half)
+        first_product(2, 0, (S,))
+        scatter_on_scalar(1, half, S)
+        nc.gpsimd.tensor_tensor(pairs[:, 0, :, 1], up[1][:], skip_sb[1], ADD)
+        scatter_on_vector(2, 0, S)
+        scatter_on_scalar(3, PLANE3_VECTOR_POINTS, S)
+
         starts = [sum(CELL_CHUNKS[:c]) for c in range(len(CELL_CHUNKS))]
         chunks = [slice(start, start + width) for start, width in zip(starts, CELL_CHUNKS)]
-        ident = keep.tile([P, P], F32, name="ident")
-        make_identity(nc, ident[:])
-        skip3_turned = keep.tile([P, REST_CELLS], F32, name="skip3_turned")
-        skip3_banks = []
-        for b, (first_chunk, last_chunk) in enumerate(ADD_GROUPS):
-            first = chunks[first_chunk].start - FIRST_CELLS
-            width = chunks[last_chunk].stop - chunks[first_chunk].start
-            turned = skip3_turned[:, first : first + width]
-            bank = psum.tile([P, BANK], F32, name="bank")
-            for block in range(0, width, P):
-                nc.tensor.transpose(
-                    bank[:, block : block + P], skip3_rest[:, first + block : first + block + P], ident[:]
-                )
-            nc.scalar.copy(turned, bank[:, :width])
-            back = held.tile([P, BANK], F32, name="held%d" % b)
-            for block in range(0, width, P):
-                nc.tensor.transpose(back[:, block : block + P], turned[:, block : block + P], ident[:])
-            skip3_banks.append(back)
-
-        z_bf = keep.tile([P, U, PACK], BF16, name="z_bf", align_bytes=64)
-        z01 = keep.tile([P, 2, U], BF16, name="z01")
-        z23 = z23_skip2[:, : REST_CELLS + 2 * FIRST_CELLS].bitcast(BF16).rearrange("p (e v) -> p e v", e=2)
-        for piece in early_pieces:
-            scatter(*piece)
-        nc.gpsimd.tensor_tensor(z01[:, 0, :], up[0][:], skip_sb[0], ADD)
-        cell_halves = [slice(a * U // 2, (a + 1) * U // 2) for a in range(2)]
-        for cells in cell_halves:
-            nc.gpsimd.tensor_tensor(z01[:, 1, cells], up[1][:, cells], skip_sb[1][:, cells], ADD)
-        scatter(*piece2)
-        nc.gpsimd.tensor_tensor(z_bf[:, :FIRST_CELLS, 2], up[2][:, :FIRST_CELLS], skip_sb[2][:, :FIRST_CELLS], ADD)
-        nc.gpsimd.tensor_tensor(z23[:, 0, :REST_CELLS], up[2][:, FIRST_CELLS:], skip_sb[2][:, FIRST_CELLS:], ADD)
-        scatter(*piece3)
-        for cells in cell_halves:
-            nc.scalar.copy(z_bf[:, cells, 0:2], z01[:, :, cells].rearrange("p e v -> p v e"))
-
         out_rows = out.rearrange("(g p) v -> p g v", p=P)
         res = keep.tile([P, OUT_TILES, U], F32, name="res")
         on_vector, on_scalar = nc.vector.tensor_copy, nc.scalar.copy
+        pair_rows = pair_words[:].rearrange("p (u v) -> p v u", u=2)
+        z_words = [keep.tile([P, 2 * width], F32, name="z_words%d" % c, align_bytes=64) for c, width in enumerate(CELL_CHUNKS)]
 
-        def add_plane3(b):
-            first, last = ADD_GROUPS[b]
-            start, stop = chunks[first].start - FIRST_CELLS, chunks[last].stop - FIRST_CELLS
-            nc.vector.tensor_tensor(
-                z23[:, 1, start:stop],
-                up[3][:, start + FIRST_CELLS : stop + FIRST_CELLS],
-                skip3_banks[b][:, : stop - start],
-                ADD,
-            )
+        def add_plane(t, first, last):
+            cells = slice(chunks[first].start, chunks[last].stop)
+            nc.vector.tensor_tensor(pairs[:, 1, cells, t - 2], up[t][:, cells], skip_sb[t][:, cells], ADD)
 
-        def weave23(c, move):
-            inner = slice(chunks[c].start - FIRST_CELLS, chunks[c].stop - FIRST_CELLS)
-            move(z_bf[:, chunks[c], 2:4], z23[:, :, inner].rearrange("p e v -> p v e"))
+        def weave(c, move):
+            move(z_words[c][:].rearrange("p (v u) -> p v u", u=2), pair_rows[:, chunks[c], :])
 
         def second_product(c, banks):
             width = CELL_CHUNKS[c]
             z_codes = keep.tile([P, width], U32, name="z_codes%d" % c, align_bytes=64)
             z_sc = keep.tile([P, width], U8, name="z_sc%d" % c, align_bytes=64)
-            nc.vector.quantize_mx(
-                out=z_codes[:].bitcast(FP8X4),
-                scales=z_sc[:],
-                in_=z_bf[:, chunks[c], :].rearrange("p v t -> p (v t)"),
-            )
+            nc.vector.quantize_mx(out=z_codes[:].bitcast(FP8X4), scales=z_sc[:], in_=z_words[c][:].bitcast(BF16))
             per_bank = OUT_TILES // banks
             sums = []
             for b in range(banks):
-                if c >= len(CELL_CHUNKS) - len(ADD_GROUPS) and b == 0:
-                    bank = held.tile([P, BANK], F32, name="held%d" % ((c + 1) % len(ADD_GROUPS)))
-                else:
-                    bank = psum.tile([P, BANK], F32, name="bank")
+                bank = psum.tile([P, BANK], F32, name="bank")
                 for place in range(per_bank):
                     g = b * per_bank + place
                     nc.tensor.matmul_mx(
@@ -253,20 +216,27 @@ def tile_picked_unet_none_e_kernel(
             for g in range(OUT_TILES):
                 store(first, last, slice(g, g + 1))
 
-        nc.gpsimd.tensor_tensor(z_bf[:, :FIRST_CELLS, 3], up[3][:, :FIRST_CELLS], skip3_first[:], ADD)
-        add_plane3(0)
-        add_plane3(1)
-        weave23(1, on_vector)
-        weave23(2, on_scalar)
-        weave23(3, on_scalar)
-        unload(0, second_product(0, 1), on_scalar)
+        add_plane(2, 0, 0)
+        add_plane(2, 1, 1)
+        add_plane(3, 0, 0)
+        add_plane(3, 1, 1)
+        weave(0, on_scalar)
+        weave(1, on_scalar)
+        add_plane(2, 2, 2)
+        sums0 = second_product(0, 1)
+        add_plane(3, 2, 2)
+        weave(2, on_scalar)
+        unload(0, sums0, on_scalar)
         store(0, 0, slice(0, OUT_TILES))
-        unload(1, second_product(1, 2), on_scalar, on_scalar)
+        add_plane(2, 3, 5)
+        sums1 = second_product(1, 2)
+        add_plane(3, 3, 5)
+        unload(1, sums1, on_scalar, on_scalar)
         store_by_tile(1, 1)
-        add_plane3(2)
+        weave(3, on_scalar)
+        weave(4, on_scalar)
         sums2 = second_product(2, 2)
-        weave23(4, on_vector)
-        weave23(5, on_vector)
+        weave(5, on_vector)
         sums3 = second_product(3, 1)
         sums4 = second_product(4, 1)
         sums5 = second_product(5, 2)

@@ -26,7 +26,8 @@ OUT_TILES = N // P
 FIRST_POINTS = 128
 REST_POINTS = (128, 256)
 W1_VECTOR_PAIRS = 40
-PLANE3_VECTOR_POINTS = 128
+PLANE2_VECTOR_POINTS = 384
+GPSIMD_CELLS = U - 192
 CELL_CHUNKS = (128, 256, 256, 128, 128, 128)
 
 
@@ -51,11 +52,13 @@ def tile_picked_unet_none_e_kernel(
         nc.sync.dma_start(cell_sb[:], cell)
 
         skip_rows = skip.rearrange("(p t) v -> p t v", t=PACK)
-        pair_words = keep.tile([P, 2 * U], F32, name="pair_words")
+        pair_words = keep.tile([P, 3 * U], F32, name="pair_words")
         skip_sb = []
         for t in range(PACK):
-            if t == 1:
-                plane = pair_words[:, U:]
+            if t == 0:
+                plane = pair_words[:, GPSIMD_CELLS : GPSIMD_CELLS + U]
+            elif t == 1:
+                plane = pair_words[:, 2 * U :]
             else:
                 plane = keep.tile([P, U], F32, name="skip_sb%d" % t)[:]
             nc.sync.dma_start(plane, skip_rows[:, t, :])
@@ -148,29 +151,36 @@ def tile_picked_unet_none_e_kernel(
             entries = cell_sb[:, start // LIST_ROWS : stop // LIST_ROWS]
             nc.scalar.activation(up[t][:].indirect(entries), h[t][:, start:stop], COPY)
 
-        pairs = pair_words[:].bitcast(BF16).rearrange("p (u v e) -> p u v e", u=2, e=2)
+        pairs = pair_words[:].bitcast(BF16).rearrange("p (u v e) -> p u v e", u=3, e=2)[:, 0:3:2]
 
         first_product(0, 0, (FIRST_POINTS,))
         scatter_on_vector(0, 0, FIRST_POINTS)
         first_product(0, FIRST_POINTS, REST_POINTS)
         scatter_on_vector(0, FIRST_POINTS, S)
-        nc.gpsimd.tensor_tensor(pairs[:, 0, :, 0], up[0][:], skip_sb[0], ADD)
+        nc.gpsimd.tensor_tensor(
+            pairs[:, 0, :GPSIMD_CELLS, 0], up[0][:, :GPSIMD_CELLS], skip_sb[0][:, :GPSIMD_CELLS], ADD
+        )
         first_product(1, 0, (S,))
-        first_product(3, 0, (S,))
-        scatter_on_vector(3, 0, PLANE3_VECTOR_POINTS)
-        scatter_on_scalar(1, 0, half)
         first_product(2, 0, (S,))
+        scatter_on_vector(2, 0, PLANE2_VECTOR_POINTS)
+        scatter_on_scalar(1, 0, half)
+        first_product(3, 0, (S,))
         scatter_on_scalar(1, half, S)
-        nc.gpsimd.tensor_tensor(pairs[:, 0, :, 1], up[1][:], skip_sb[1], ADD)
-        scatter_on_vector(2, 0, S)
-        scatter_on_scalar(3, PLANE3_VECTOR_POINTS, S)
+        nc.vector.tensor_tensor(pairs[:, 0, :, 1], up[1][:], skip_sb[1], ADD)
+        nc.vector.tensor_tensor(
+            pairs[:, 0, GPSIMD_CELLS:, 0], up[0][:, GPSIMD_CELLS:], skip_sb[0][:, GPSIMD_CELLS:], ADD
+        )
+        scatter_on_scalar(3, 0, FIRST_POINTS)
+        scatter_on_scalar(2, PLANE2_VECTOR_POINTS, S)
+        nc.vector.tensor_tensor(pairs[:, 1, :, 0], up[2][:], skip_sb[2], ADD)
+        scatter_on_scalar(3, FIRST_POINTS, S)
 
         starts = [sum(CELL_CHUNKS[:c]) for c in range(len(CELL_CHUNKS))]
         chunks = [slice(start, start + width) for start, width in zip(starts, CELL_CHUNKS)]
         out_rows = out.rearrange("(g p) v -> p g v", p=P)
         res = keep.tile([P, OUT_TILES, U], F32, name="res")
         on_vector, on_scalar = nc.vector.tensor_copy, nc.scalar.copy
-        pair_rows = pair_words[:].rearrange("p (u v) -> p v u", u=2)
+        pair_rows = pair_words[:].rearrange("p (u v) -> p v u", u=3)[:, :, 0:3:2]
         z_words = [keep.tile([P, 2 * width], F32, name="z_words%d" % c, align_bytes=64) for c, width in enumerate(CELL_CHUNKS)]
 
         def add_plane(t, first, last):
@@ -216,27 +226,24 @@ def tile_picked_unet_none_e_kernel(
             for g in range(OUT_TILES):
                 store(first, last, slice(g, g + 1))
 
-        add_plane(2, 0, 0)
-        add_plane(2, 1, 1)
         add_plane(3, 0, 0)
         add_plane(3, 1, 1)
         weave(0, on_scalar)
         weave(1, on_scalar)
-        add_plane(2, 2, 2)
-        sums0 = second_product(0, 1)
         add_plane(3, 2, 2)
         weave(2, on_scalar)
+        sums0 = second_product(0, 1)
+        add_plane(3, 3, 3)
+        sums1 = second_product(1, 2)
+        add_plane(3, 4, 5)
+        weave(3, on_scalar)
         unload(0, sums0, on_scalar)
         store(0, 0, slice(0, OUT_TILES))
-        add_plane(2, 3, 5)
-        sums1 = second_product(1, 2)
-        add_plane(3, 3, 5)
-        unload(1, sums1, on_scalar, on_scalar)
-        store_by_tile(1, 1)
-        weave(3, on_scalar)
         weave(4, on_scalar)
         sums2 = second_product(2, 2)
         weave(5, on_vector)
+        unload(1, sums1, on_scalar, on_scalar)
+        store_by_tile(1, 1)
         sums3 = second_product(3, 1)
         sums4 = second_product(4, 1)
         sums5 = second_product(5, 2)

@@ -28,6 +28,7 @@ REST_POINTS = (128, 256)
 W1_VECTOR_PAIRS = 40
 PLANE2_VECTOR_POINTS = 384
 GPSIMD_CELLS = U - 192
+LATE_CELLS = 256
 CELL_CHUNKS = (128, 256, 256, 128, 128, 128)
 
 
@@ -61,7 +62,8 @@ def tile_picked_unet_none_e_kernel(
                 plane = pair_words[:, 2 * U :]
             else:
                 plane = keep.tile([P, U], F32, name="skip_sb%d" % t)[:]
-            nc.sync.dma_start(plane, skip_rows[:, t, :])
+            cells = slice(0, U - LATE_CELLS if t == 3 else U)
+            nc.sync.dma_start(plane[:, cells], skip_rows[:, t, cells])
             skip_sb.append(plane)
 
         w2_codes = keep.tile([P, N], I32, name="w2_codes", align_bytes=64)
@@ -170,6 +172,8 @@ def tile_picked_unet_none_e_kernel(
         nc.vector.tensor_tensor(
             pairs[:, 0, GPSIMD_CELLS:, 0], up[0][:, GPSIMD_CELLS:], skip_sb[0][:, GPSIMD_CELLS:], ADD
         )
+        skip3_late = skip_sb[0][:, U - LATE_CELLS :]
+        nc.sync.dma_start(skip3_late, skip_rows[:, 3, U - LATE_CELLS :])
         scatter_on_scalar(3, 0, FIRST_POINTS)
         scatter_on_scalar(2, PLANE2_VECTOR_POINTS, S)
         nc.vector.tensor_tensor(pairs[:, 1, :, 0], up[2][:], skip_sb[2], ADD)
@@ -235,7 +239,7 @@ def tile_picked_unet_none_e_kernel(
         sums0 = second_product(0, 1)
         add_plane(3, 3, 3)
         sums1 = second_product(1, 2)
-        add_plane(3, 4, 5)
+        nc.vector.tensor_tensor(pairs[:, 1, U - LATE_CELLS :, 1], up[3][:, U - LATE_CELLS :], skip3_late, ADD)
         weave(3, on_scalar)
         unload(0, sums0, on_scalar)
         store(0, 0, slice(0, OUT_TILES))
@@ -251,5 +255,6 @@ def tile_picked_unet_none_e_kernel(
         store_by_tile(2, 2)
         unload(3, sums3, on_scalar)
         unload(4, sums4, on_vector)
+        store_by_tile(3, 4)
         unload(5, sums5, on_scalar, on_vector)
-        store_by_tile(3, 5)
+        store(5, 5, slice(0, OUT_TILES))

@@ -26,8 +26,9 @@ OUT_TILES = N // P
 FIRST_POINTS = 128
 REST_POINTS = (128, 256)
 W1_VECTOR_PAIRS = 40
-PLANE2_VECTOR_POINTS = 384
-GPSIMD_CELLS = U - 192
+PLANE1_VECTOR_POINTS = 384
+PLANE3_FIRST_POINTS = 192
+GPSIMD_CELLS = U - 16
 LATE_CELLS = 256
 CELL_CHUNKS = (128, 256, 256, 128, 128, 128)
 
@@ -54,17 +55,15 @@ def tile_picked_unet_none_e_kernel(
 
         skip_rows = skip.rearrange("(p t) v -> p t v", t=PACK)
         pair_words = keep.tile([P, 3 * U], F32, name="pair_words")
-        skip_sb = []
-        for t in range(PACK):
+        skip_sb = {}
+        for t in (0, 2, 1, 3):
             if t == 0:
                 plane = pair_words[:, GPSIMD_CELLS : GPSIMD_CELLS + U]
-            elif t == 1:
-                plane = pair_words[:, 2 * U :]
             else:
                 plane = keep.tile([P, U], F32, name="skip_sb%d" % t)[:]
-            cells = slice(0, U - LATE_CELLS if t == 3 else U)
+            cells = slice(0, {0: GPSIMD_CELLS, 3: U - LATE_CELLS}.get(t, U))
             nc.sync.dma_start(plane[:, cells], skip_rows[:, t, cells])
-            skip_sb.append(plane)
+            skip_sb.setdefault(t, plane)
 
         w2_codes = keep.tile([P, N], I32, name="w2_codes", align_bytes=64)
         nc.sync.dma_start(w2_codes[:], w2_words[0].rearrange("p n r -> p (n r)").bitcast(I32))
@@ -128,7 +127,7 @@ def tile_picked_unet_none_e_kernel(
 
         h = [keep.tile([P, S], F32, name="h%d" % t) for t in range(PACK)]
 
-        def first_product(t, start, widths):
+        def first_product(t, start, widths, move=nc.scalar.copy):
             bank = psum.tile([P, BANK], F32, name="bank")
             done = 0
             for width in widths:
@@ -143,7 +142,7 @@ def tile_picked_unet_none_e_kernel(
                     stop=True,
                 )
                 done = done + width
-            nc.scalar.copy(h[t][:, start : start + done], bank[:, :done])
+            move(h[t][:, start : start + done], bank[:, :done])
 
         def scatter_on_vector(t, start, stop):
             entries = cell_sb[:, start // LIST_ROWS : stop // LIST_ROWS]
@@ -158,26 +157,26 @@ def tile_picked_unet_none_e_kernel(
         first_product(0, 0, (FIRST_POINTS,))
         scatter_on_vector(0, 0, FIRST_POINTS)
         first_product(0, FIRST_POINTS, REST_POINTS)
+        first_product(2, 0, (half,))
+        first_product(2, half, (half,), nc.vector.tensor_copy)
         scatter_on_vector(0, FIRST_POINTS, S)
         nc.gpsimd.tensor_tensor(
             pairs[:, 0, :GPSIMD_CELLS, 0], up[0][:, :GPSIMD_CELLS], skip_sb[0][:, :GPSIMD_CELLS], ADD
         )
         first_product(1, 0, (S,))
-        first_product(2, 0, (S,))
-        scatter_on_vector(2, 0, PLANE2_VECTOR_POINTS)
-        scatter_on_scalar(1, 0, half)
+        scatter_on_vector(1, 0, PLANE1_VECTOR_POINTS)
+        scatter_on_scalar(2, 0, half)
         first_product(3, 0, (S,))
-        scatter_on_scalar(1, half, S)
-        nc.vector.tensor_tensor(pairs[:, 0, :, 1], up[1][:], skip_sb[1], ADD)
-        nc.vector.tensor_tensor(
-            pairs[:, 0, GPSIMD_CELLS:, 0], up[0][:, GPSIMD_CELLS:], skip_sb[0][:, GPSIMD_CELLS:], ADD
-        )
-        skip3_late = skip_sb[0][:, U - LATE_CELLS :]
-        nc.sync.dma_start(skip3_late, skip_rows[:, 3, U - LATE_CELLS :])
-        scatter_on_scalar(3, 0, FIRST_POINTS)
-        scatter_on_scalar(2, PLANE2_VECTOR_POINTS, S)
+        scatter_on_scalar(2, half, S)
         nc.vector.tensor_tensor(pairs[:, 1, :, 0], up[2][:], skip_sb[2], ADD)
-        scatter_on_scalar(3, FIRST_POINTS, S)
+        skip3_late = skip_sb[0][:, GPSIMD_CELLS - LATE_CELLS : GPSIMD_CELLS]
+        nc.sync.dma_start(skip3_late, skip_rows[:, 3, U - LATE_CELLS :])
+        skip0_late = skip_sb[0][:, U - GPSIMD_CELLS : 2 * (U - GPSIMD_CELLS)]
+        nc.sync.dma_start(skip0_late, skip_rows[:, 0, GPSIMD_CELLS:])
+        scatter_on_scalar(3, 0, PLANE3_FIRST_POINTS)
+        scatter_on_scalar(1, PLANE1_VECTOR_POINTS, S)
+        nc.vector.tensor_tensor(pairs[:, 0, :, 1], up[1][:], skip_sb[1], ADD)
+        scatter_on_scalar(3, PLANE3_FIRST_POINTS, S)
 
         starts = [sum(CELL_CHUNKS[:c]) for c in range(len(CELL_CHUNKS))]
         chunks = [slice(start, start + width) for start, width in zip(starts, CELL_CHUNKS)]
@@ -185,20 +184,21 @@ def tile_picked_unet_none_e_kernel(
         res = keep.tile([P, OUT_TILES, U], F32, name="res")
         on_vector, on_scalar = nc.vector.tensor_copy, nc.scalar.copy
         pair_rows = pair_words[:].rearrange("p (u v) -> p v u", u=3)[:, :, 0:3:2]
-        z_words = [keep.tile([P, 2 * width], F32, name="z_words%d" % c, align_bytes=64) for c, width in enumerate(CELL_CHUNKS)]
+        z_words = keep.tile([P, 2 * U], F32, name="z_words", align_bytes=64)
 
         def add_plane(t, first, last):
             cells = slice(chunks[first].start, chunks[last].stop)
             nc.vector.tensor_tensor(pairs[:, 1, cells, t - 2], up[t][:, cells], skip_sb[t][:, cells], ADD)
 
-        def weave(c, move):
-            move(z_words[c][:].rearrange("p (v u) -> p v u", u=2), pair_rows[:, chunks[c], :])
+        def weave(first, last, move):
+            cells = slice(chunks[first].start, chunks[last].stop)
+            move(z_words[:].rearrange("p (v u) -> p v u", u=2)[:, cells, :], pair_rows[:, cells, :])
 
         def second_product(c, banks):
             width = CELL_CHUNKS[c]
             z_codes = keep.tile([P, width], U32, name="z_codes%d" % c, align_bytes=64)
             z_sc = keep.tile([P, width], U8, name="z_sc%d" % c, align_bytes=64)
-            nc.vector.quantize_mx(out=z_codes[:].bitcast(FP8X4), scales=z_sc[:], in_=z_words[c][:].bitcast(BF16))
+            nc.vector.quantize_mx(out=z_codes[:].bitcast(FP8X4), scales=z_sc[:], in_=z_words[:, 2 * chunks[c].start : 2 * chunks[c].stop].bitcast(BF16))
             per_bank = OUT_TILES // banks
             sums = []
             for b in range(banks):
@@ -232,29 +232,30 @@ def tile_picked_unet_none_e_kernel(
 
         add_plane(3, 0, 0)
         add_plane(3, 1, 1)
-        weave(0, on_scalar)
-        weave(1, on_scalar)
+        weave(0, 0, on_scalar)
+        weave(1, 1, on_scalar)
         add_plane(3, 2, 2)
-        weave(2, on_scalar)
+        weave(2, 2, on_scalar)
         sums0 = second_product(0, 1)
         add_plane(3, 3, 3)
         sums1 = second_product(1, 2)
+        nc.vector.tensor_tensor(pairs[:, 0, GPSIMD_CELLS:, 0], up[0][:, GPSIMD_CELLS:], skip0_late, ADD)
         nc.vector.tensor_tensor(pairs[:, 1, U - LATE_CELLS :, 1], up[3][:, U - LATE_CELLS :], skip3_late, ADD)
-        weave(3, on_scalar)
+        weave(3, 3, on_scalar)
         unload(0, sums0, on_scalar)
         store(0, 0, slice(0, OUT_TILES))
-        weave(4, on_scalar)
         sums2 = second_product(2, 2)
-        weave(5, on_vector)
+        weave(4, 5, on_vector)
         unload(1, sums1, on_scalar, on_scalar)
         store_by_tile(1, 1)
         sums3 = second_product(3, 1)
         sums4 = second_product(4, 1)
         sums5 = second_product(5, 2)
-        unload(2, sums2, on_scalar, on_vector)
+        unload(2, sums2, on_scalar, on_scalar)
         store_by_tile(2, 2)
-        unload(3, sums3, on_scalar)
+        unload(3, sums3, on_vector)
+        store(3, 3, slice(0, OUT_TILES))
         unload(4, sums4, on_vector)
-        store_by_tile(3, 4)
+        store(4, 4, slice(0, OUT_TILES))
         unload(5, sums5, on_scalar, on_vector)
         store(5, 5, slice(0, OUT_TILES))

@@ -22,15 +22,13 @@ BANKS = 8
 LIST_ROWS = 16
 QUADRANT = 32
 OUT_TILES = N // P
+HALF = S // 2
 
 FIRST_POINTS = 128
-REST_POINTS = (128, 256)
+VECTOR_POINTS = 384
 W1_VECTOR_PAIRS = 40
-PLANE1_VECTOR_POINTS = 384
-PLANE3_FIRST_POINTS = 192
-GPSIMD_CELLS = U - 16
-LATE_CELLS = 256
 CELL_CHUNKS = (128, 256, 256, 128, 128, 128)
+GPSIMD_CELLS = 576
 
 
 def tile_picked_unet_none_e_kernel(
@@ -53,18 +51,6 @@ def tile_picked_unet_none_e_kernel(
         nc.sync.dma_start(w1_raw[:], w1.rearrange("(p j) c -> p j c", j=PACK))
         nc.sync.dma_start(cell_sb[:], cell)
 
-        skip_rows = skip.rearrange("(p t) v -> p t v", t=PACK)
-        pair_words = keep.tile([P, 3 * U], F32, name="pair_words")
-        skip_sb = {}
-        for t in (0, 2, 1, 3):
-            if t == 0:
-                plane = pair_words[:, GPSIMD_CELLS : GPSIMD_CELLS + U]
-            else:
-                plane = keep.tile([P, U], F32, name="skip_sb%d" % t)[:]
-            cells = slice(0, {0: GPSIMD_CELLS, 3: U - LATE_CELLS}.get(t, U))
-            nc.sync.dma_start(plane[:, cells], skip_rows[:, t, cells])
-            skip_sb.setdefault(t, plane)
-
         w2_codes = keep.tile([P, N], I32, name="w2_codes", align_bytes=64)
         nc.sync.dma_start(w2_codes[:], w2_words[0].rearrange("p n r -> p (n r)").bitcast(I32))
         w2_sc = keep.tile([P, N], U8, name="w2_sc", align_bytes=64)
@@ -75,25 +61,36 @@ def tile_picked_unet_none_e_kernel(
                 w2_scales[0, 4 * q : 4 * q + 4, :].bitcast(I32),
             )
 
+        skip_rows = skip.rearrange("(p t) v -> p t v", t=PACK)
+        pair_words = keep.tile([P, GPSIMD_CELLS + 2 * U], F32, name="pair_words")
+        skip_sb = {}
+        for t in (3, 2, 0, 1):
+            if t in (1, 2):
+                plane = pair_words[:, GPSIMD_CELLS + (t - 1) * U : GPSIMD_CELLS + t * U]
+            else:
+                plane = keep.tile([P, U], F32, name="skip_sb%d" % t)[:]
+            nc.sync.dma_start(plane, skip_rows[:, t, :])
+            skip_sb[t] = plane
+
         up = []
         for t in range(PACK):
             window = keep.tile([P, U], F32, name="up%d" % t)
             nc.vector.memset(window[:], 0.0)
             up.append(window)
 
+        def entries(list_sb, start, stop):
+            return list_sb[:, start // LIST_ROWS : stop // LIST_ROWS]
+
         x_bf = keep.tile([P, S, PACK], BF16, name="x_bf", align_bytes=64)
-        for j in range(PACK - 1):
-            nc.vector.tensor_copy(x_bf[:, :, j], x_raw[j][:].indirect(offs_sb[:]))
-        half = S // 2
-        for a in range(2):
-            nc.vector.tensor_copy(
-                x_bf[:, a * half : (a + 1) * half, PACK - 1],
-                x_raw[PACK - 1][:].indirect(offs_sb[:, a * half // LIST_ROWS : (a + 1) * half // LIST_ROWS]),
-            )
+        x_late = keep.tile([P, PACK, S - VECTOR_POINTS], BF16, name="x_late")
+        for j in range(PACK):
+            nc.vector.tensor_copy(x_bf[:, :VECTOR_POINTS, j], x_raw[j][:].indirect(entries(offs_sb, 0, VECTOR_POINTS)))
+            nc.scalar.activation(x_late[:, j, :], x_raw[j][:].indirect(entries(offs_sb, VECTOR_POINTS, S)), COPY)
+            if j % 2:
+                nc.scalar.copy(x_bf[:, VECTOR_POINTS:, j - 1 : j + 1], x_late[:, j - 1 : j + 1, :].rearrange("p e s -> p s e"))
         x_codes = keep.tile([P, S], U32, name="x_codes", align_bytes=64)
         x_sc = keep.tile([P, S], U8, name="x_sc", align_bytes=64)
-        for a in range(2):
-            points = slice(a * half, (a + 1) * half)
+        for points in (slice(VECTOR_POINTS, S), slice(0, VECTOR_POINTS)):
             nc.vector.quantize_mx(
                 out=x_codes[:, points].bitcast(FP8X4),
                 scales=x_sc[:, points],
@@ -126,8 +123,9 @@ def tile_picked_unet_none_e_kernel(
         quantize_w1(2, 4)
 
         h = [keep.tile([P, S], F32, name="h%d" % t) for t in range(PACK)]
+        on_vector, on_scalar = nc.vector.tensor_copy, nc.scalar.copy
 
-        def first_product(t, start, widths, move=nc.scalar.copy):
+        def first_product(t, start, widths, move):
             bank = psum.tile([P, BANK], F32, name="bank")
             done = 0
             for width in widths:
@@ -145,50 +143,47 @@ def tile_picked_unet_none_e_kernel(
             move(h[t][:, start : start + done], bank[:, :done])
 
         def scatter_on_vector(t, start, stop):
-            entries = cell_sb[:, start // LIST_ROWS : stop // LIST_ROWS]
-            nc.vector.tensor_copy(up[t][:].indirect(entries), h[t][:, start:stop])
+            nc.vector.tensor_copy(up[t][:].indirect(entries(cell_sb, start, stop)), h[t][:, start:stop])
 
         def scatter_on_scalar(t, start, stop):
-            entries = cell_sb[:, start // LIST_ROWS : stop // LIST_ROWS]
-            nc.scalar.activation(up[t][:].indirect(entries), h[t][:, start:stop], COPY)
+            nc.scalar.activation(up[t][:].indirect(entries(cell_sb, start, stop)), h[t][:, start:stop], COPY)
 
-        pairs = pair_words[:].bitcast(BF16).rearrange("p (u v e) -> p u v e", u=3, e=2)[:, 0:3:2]
+        pairs = pair_words[:, : 2 * U].bitcast(BF16).rearrange("p (u v e) -> p u v e", u=2, e=2)
 
-        first_product(0, 0, (FIRST_POINTS,))
+        def add_plane(engine, t, start, stop):
+            engine.tensor_tensor(
+                pairs[:, t // 2, start:stop, t % 2], up[t][:, start:stop], skip_sb[t][:, start:stop], ADD
+            )
+
+        first_product(0, 0, (FIRST_POINTS,), on_scalar)
         scatter_on_vector(0, 0, FIRST_POINTS)
-        first_product(0, FIRST_POINTS, REST_POINTS)
-        first_product(2, 0, (half,))
-        first_product(2, half, (half,), nc.vector.tensor_copy)
+        first_product(0, FIRST_POINTS, (FIRST_POINTS, HALF), on_scalar)
+        first_product(1, 0, (HALF,), on_scalar)
+        first_product(2, 0, (HALF,), on_vector)
         scatter_on_vector(0, FIRST_POINTS, S)
-        nc.gpsimd.tensor_tensor(
-            pairs[:, 0, :GPSIMD_CELLS, 0], up[0][:, :GPSIMD_CELLS], skip_sb[0][:, :GPSIMD_CELLS], ADD
-        )
-        first_product(1, 0, (S,))
-        scatter_on_vector(1, 0, PLANE1_VECTOR_POINTS)
-        scatter_on_scalar(2, 0, half)
-        first_product(3, 0, (S,))
-        scatter_on_scalar(2, half, S)
-        nc.vector.tensor_tensor(pairs[:, 1, :, 0], up[2][:], skip_sb[2], ADD)
-        skip3_late = skip_sb[0][:, GPSIMD_CELLS - LATE_CELLS : GPSIMD_CELLS]
-        nc.sync.dma_start(skip3_late, skip_rows[:, 3, U - LATE_CELLS :])
-        skip0_late = skip_sb[0][:, U - GPSIMD_CELLS : 2 * (U - GPSIMD_CELLS)]
-        nc.sync.dma_start(skip0_late, skip_rows[:, 0, GPSIMD_CELLS:])
-        scatter_on_scalar(3, 0, PLANE3_FIRST_POINTS)
-        scatter_on_scalar(1, PLANE1_VECTOR_POINTS, S)
-        nc.vector.tensor_tensor(pairs[:, 0, :, 1], up[1][:], skip_sb[1], ADD)
-        scatter_on_scalar(3, PLANE3_FIRST_POINTS, S)
+        add_plane(nc.gpsimd, 0, 0, GPSIMD_CELLS)
+        first_product(2, HALF, (HALF,), on_scalar)
+        scatter_on_scalar(1, 0, HALF)
+        scatter_on_vector(2, 0, S)
+        first_product(1, HALF, (HALF,), on_scalar)
+        scatter_on_scalar(1, HALF, S)
+        add_plane(nc.gpsimd, 1, 0, GPSIMD_CELLS)
+        first_product(3, 0, (HALF,), on_scalar)
+        scatter_on_scalar(3, 0, HALF)
+        first_product(3, HALF, (HALF,), on_scalar)
+        scatter_on_scalar(3, HALF, S)
+        add_plane(nc.vector, 1, GPSIMD_CELLS, U)
+        add_plane(nc.vector, 0, GPSIMD_CELLS, U)
 
         starts = [sum(CELL_CHUNKS[:c]) for c in range(len(CELL_CHUNKS))]
         chunks = [slice(start, start + width) for start, width in zip(starts, CELL_CHUNKS)]
         out_rows = out.rearrange("(g p) v -> p g v", p=P)
         res = keep.tile([P, OUT_TILES, U], F32, name="res")
-        on_vector, on_scalar = nc.vector.tensor_copy, nc.scalar.copy
-        pair_rows = pair_words[:].rearrange("p (u v) -> p v u", u=3)[:, :, 0:3:2]
+        pair_rows = pair_words[:, : 2 * U].rearrange("p (u v) -> p v u", u=2)
         z_words = keep.tile([P, 2 * U], F32, name="z_words", align_bytes=64)
 
-        def add_plane(t, first, last):
-            cells = slice(chunks[first].start, chunks[last].stop)
-            nc.vector.tensor_tensor(pairs[:, 1, cells, t - 2], up[t][:, cells], skip_sb[t][:, cells], ADD)
+        def add_chunks(t, first, last):
+            add_plane(nc.vector, t, chunks[first].start, chunks[last].stop)
 
         def weave(first, last, move):
             cells = slice(chunks[first].start, chunks[last].stop)
@@ -198,7 +193,11 @@ def tile_picked_unet_none_e_kernel(
             width = CELL_CHUNKS[c]
             z_codes = keep.tile([P, width], U32, name="z_codes%d" % c, align_bytes=64)
             z_sc = keep.tile([P, width], U8, name="z_sc%d" % c, align_bytes=64)
-            nc.vector.quantize_mx(out=z_codes[:].bitcast(FP8X4), scales=z_sc[:], in_=z_words[:, 2 * chunks[c].start : 2 * chunks[c].stop].bitcast(BF16))
+            nc.vector.quantize_mx(
+                out=z_codes[:].bitcast(FP8X4),
+                scales=z_sc[:],
+                in_=z_words[:, 2 * chunks[c].start : 2 * chunks[c].stop].bitcast(BF16),
+            )
             per_bank = OUT_TILES // banks
             sums = []
             for b in range(banks):
@@ -222,40 +221,43 @@ def tile_picked_unet_none_e_kernel(
             for b, (bank_sums, move) in enumerate(zip(sums, moves)):
                 move(res[:, b * per_bank : (b + 1) * per_bank, chunks[c]], bank_sums)
 
-        def store(first, last, tiles):
-            cells = slice(chunks[first].start, chunks[last].stop)
-            nc.sync.dma_start(out_rows[:, tiles, cells], res[:, tiles, cells])
+        def store(c, tiles):
+            nc.sync.dma_start(out_rows[:, tiles, chunks[c]], res[:, tiles, chunks[c]])
 
-        def store_by_tile(first, last):
+        def store_by_tile(c):
             for g in range(OUT_TILES):
-                store(first, last, slice(g, g + 1))
+                store(c, slice(g, g + 1))
 
-        add_plane(3, 0, 0)
-        add_plane(3, 1, 1)
+        both = slice(0, OUT_TILES)
+
+        add_chunks(2, 0, 1)
+        add_chunks(3, 0, 0)
+        add_chunks(3, 1, 1)
         weave(0, 0, on_scalar)
         weave(1, 1, on_scalar)
-        add_plane(3, 2, 2)
-        weave(2, 2, on_scalar)
+        add_chunks(2, 2, 2)
         sums0 = second_product(0, 1)
-        add_plane(3, 3, 3)
-        sums1 = second_product(1, 2)
-        nc.vector.tensor_tensor(pairs[:, 0, GPSIMD_CELLS:, 0], up[0][:, GPSIMD_CELLS:], skip0_late, ADD)
-        nc.vector.tensor_tensor(pairs[:, 1, U - LATE_CELLS :, 1], up[3][:, U - LATE_CELLS :], skip3_late, ADD)
-        weave(3, 3, on_scalar)
+        add_chunks(3, 2, 2)
         unload(0, sums0, on_scalar)
-        store(0, 0, slice(0, OUT_TILES))
+        store(0, both)
+        weave(2, 2, on_scalar)
+        sums1 = second_product(1, 2)
+        add_chunks(2, 3, 5)
+        add_chunks(3, 3, 3)
+        add_chunks(3, 4, 5)
+        unload(1, sums1, on_scalar, on_scalar)
+        store_by_tile(1)
+        weave(3, 3, on_scalar)
         sums2 = second_product(2, 2)
         weave(4, 5, on_vector)
-        unload(1, sums1, on_scalar, on_scalar)
-        store_by_tile(1, 1)
         sums3 = second_product(3, 1)
         sums4 = second_product(4, 1)
         sums5 = second_product(5, 2)
         unload(2, sums2, on_scalar, on_scalar)
-        store_by_tile(2, 2)
+        store_by_tile(2)
         unload(3, sums3, on_vector)
-        store(3, 3, slice(0, OUT_TILES))
+        store(3, both)
         unload(4, sums4, on_vector)
-        store(4, 4, slice(0, OUT_TILES))
+        store(4, both)
         unload(5, sums5, on_scalar, on_vector)
-        store(5, 5, slice(0, OUT_TILES))
+        store(5, both)

@@ -28,7 +28,9 @@ FIRST_POINTS = 128
 VECTOR_POINTS = 384
 W1_VECTOR_PAIRS = 40
 CELL_CHUNKS = (128, 256, 256, 128, 128, 128)
-GPSIMD_CELLS = 576
+GPSIMD_CELLS = 192
+FIRST_CELLS = 256
+WALK = 4
 
 
 def tile_picked_unet_none_e_kernel(
@@ -62,11 +64,12 @@ def tile_picked_unet_none_e_kernel(
             )
 
         skip_rows = skip.rearrange("(p t) v -> p t v", t=PACK)
-        pair_words = keep.tile([P, GPSIMD_CELLS + 2 * U], F32, name="pair_words")
+        skip1_start = U + FIRST_CELLS // 2 - GPSIMD_CELLS
+        sum_words = keep.tile([P, skip1_start + 2 * U], F32, name="sum_words")
         skip_sb = {}
         for t in (3, 2, 0, 1):
             if t in (1, 2):
-                plane = pair_words[:, GPSIMD_CELLS + (t - 1) * U : GPSIMD_CELLS + t * U]
+                plane = sum_words[:, skip1_start + (t - 1) * U : skip1_start + t * U]
             else:
                 plane = keep.tile([P, U], F32, name="skip_sb%d" % t)[:]
             nc.sync.dma_start(plane, skip_rows[:, t, :])
@@ -148,11 +151,11 @@ def tile_picked_unet_none_e_kernel(
         def scatter_on_scalar(t, start, stop):
             nc.scalar.activation(up[t][:].indirect(entries(cell_sb, start, stop)), h[t][:, start:stop], COPY)
 
-        pairs = pair_words[:, : 2 * U].bitcast(BF16).rearrange("p (u v e) -> p u v e", u=2, e=2)
+        sums = sum_words[:, : 2 * U].bitcast(BF16)
 
         def add_plane(engine, t, start, stop):
             engine.tensor_tensor(
-                pairs[:, t // 2, start:stop, t % 2], up[t][:, start:stop], skip_sb[t][:, start:stop], ADD
+                sums[:, t * U + start : t * U + stop], up[t][:, start:stop], skip_sb[t][:, start:stop], ADD
             )
 
         first_product(0, 0, (FIRST_POINTS,), on_scalar)
@@ -161,7 +164,7 @@ def tile_picked_unet_none_e_kernel(
         first_product(1, 0, (HALF,), on_scalar)
         first_product(2, 0, (HALF,), on_vector)
         scatter_on_vector(0, FIRST_POINTS, S)
-        add_plane(nc.gpsimd, 0, 0, GPSIMD_CELLS)
+        add_plane(nc.gpsimd, 0, 0, U)
         first_product(2, HALF, (HALF,), on_scalar)
         scatter_on_scalar(1, 0, HALF)
         scatter_on_vector(2, 0, S)
@@ -173,21 +176,21 @@ def tile_picked_unet_none_e_kernel(
         first_product(3, HALF, (HALF,), on_scalar)
         scatter_on_scalar(3, HALF, S)
         add_plane(nc.vector, 1, GPSIMD_CELLS, U)
-        add_plane(nc.vector, 0, GPSIMD_CELLS, U)
 
         starts = [sum(CELL_CHUNKS[:c]) for c in range(len(CELL_CHUNKS))]
         chunks = [slice(start, start + width) for start, width in zip(starts, CELL_CHUNKS)]
         out_rows = out.rearrange("(g p) v -> p g v", p=P)
         res = keep.tile([P, OUT_TILES, U], F32, name="res")
-        pair_rows = pair_words[:, : 2 * U].rearrange("p (u v) -> p v u", u=2)
-        z_words = keep.tile([P, 2 * U], F32, name="z_words", align_bytes=64)
+        z_bf = keep.tile([P, U * PACK], BF16, name="z_bf", align_bytes=64)
+        weave_src = sums.rearrange("p (t c i) -> p c t i", t=PACK, i=WALK)
+        weave_dst = z_bf[:].rearrange("p (c i t) -> p c t i", t=PACK, i=WALK)
 
         def add_chunks(t, first, last):
             add_plane(nc.vector, t, chunks[first].start, chunks[last].stop)
 
         def weave(first, last, move):
-            cells = slice(chunks[first].start, chunks[last].stop)
-            move(z_words[:].rearrange("p (v u) -> p v u", u=2)[:, cells, :], pair_rows[:, cells, :])
+            runs = slice(chunks[first].start // WALK, chunks[last].stop // WALK)
+            move(weave_dst[:, runs], weave_src[:, runs])
 
         def second_product(c, banks):
             width = CELL_CHUNKS[c]
@@ -196,10 +199,10 @@ def tile_picked_unet_none_e_kernel(
             nc.vector.quantize_mx(
                 out=z_codes[:].bitcast(FP8X4),
                 scales=z_sc[:],
-                in_=z_words[:, 2 * chunks[c].start : 2 * chunks[c].stop].bitcast(BF16),
+                in_=z_bf[:, PACK * chunks[c].start : PACK * chunks[c].stop],
             )
             per_bank = OUT_TILES // banks
-            sums = []
+            parts = []
             for b in range(banks):
                 bank = psum.tile([P, BANK], F32, name="bank")
                 for place in range(per_bank):
@@ -213,12 +216,12 @@ def tile_picked_unet_none_e_kernel(
                         start=True,
                         stop=True,
                     )
-                sums.append(bank[:, : per_bank * width].rearrange("p (g v) -> p g v", g=per_bank))
-            return sums
+                parts.append(bank[:, : per_bank * width].rearrange("p (g v) -> p g v", g=per_bank))
+            return parts
 
-        def unload(c, sums, *moves):
-            per_bank = OUT_TILES // len(sums)
-            for b, (bank_sums, move) in enumerate(zip(sums, moves)):
+        def unload(c, parts, *moves):
+            per_bank = OUT_TILES // len(parts)
+            for b, (bank_sums, move) in enumerate(zip(parts, moves)):
                 move(res[:, b * per_bank : (b + 1) * per_bank, chunks[c]], bank_sums)
 
         def store(c, tiles):
@@ -230,32 +233,30 @@ def tile_picked_unet_none_e_kernel(
 
         both = slice(0, OUT_TILES)
 
-        add_chunks(2, 0, 1)
+        add_plane(nc.vector, 2, 0, FIRST_CELLS)
+        add_plane(nc.vector, 2, FIRST_CELLS, U)
         add_chunks(3, 0, 0)
         add_chunks(3, 1, 1)
-        weave(0, 0, on_scalar)
+        weave(0, 0, on_vector)
         weave(1, 1, on_scalar)
-        add_chunks(2, 2, 2)
+        add_chunks(3, 2, 3)
         sums0 = second_product(0, 1)
-        add_chunks(3, 2, 2)
+        weave(3, 3, on_scalar)
+        weave(2, 2, on_vector)
         unload(0, sums0, on_scalar)
         store(0, both)
-        weave(2, 2, on_scalar)
         sums1 = second_product(1, 2)
-        add_chunks(2, 3, 5)
-        add_chunks(3, 3, 3)
         add_chunks(3, 4, 5)
-        unload(1, sums1, on_scalar, on_scalar)
-        store_by_tile(1)
-        weave(3, 3, on_scalar)
         sums2 = second_product(2, 2)
         weave(4, 5, on_vector)
+        unload(1, sums1, on_scalar, on_scalar)
+        store_by_tile(1)
         sums3 = second_product(3, 1)
         sums4 = second_product(4, 1)
         sums5 = second_product(5, 2)
         unload(2, sums2, on_scalar, on_scalar)
         store_by_tile(2)
-        unload(3, sums3, on_vector)
+        unload(3, sums3, on_scalar)
         store(3, both)
         unload(4, sums4, on_vector)
         store(4, both)

@@ -160,18 +160,18 @@ def tile_picked_unet_none_e_kernel(
 
         first_product(0, 0, (FIRST_POINTS,), on_scalar)
         scatter_on_vector(0, 0, FIRST_POINTS)
-        first_product(0, FIRST_POINTS, (FIRST_POINTS, HALF), on_scalar)
         first_product(1, 0, (HALF,), on_scalar)
+        first_product(0, FIRST_POINTS, (FIRST_POINTS, HALF), on_scalar)
+        scatter_on_scalar(1, 0, HALF)
         first_product(2, 0, (HALF,), on_vector)
         scatter_on_vector(0, FIRST_POINTS, S)
         add_plane(nc.gpsimd, 0, 0, U)
-        first_product(2, HALF, (HALF,), on_scalar)
-        scatter_on_scalar(1, 0, HALF)
-        scatter_on_vector(2, 0, S)
         first_product(1, HALF, (HALF,), on_scalar)
+        first_product(2, HALF, (HALF,), on_scalar)
+        scatter_on_vector(2, 0, S)
+        first_product(3, 0, (HALF,), on_scalar)
         scatter_on_scalar(1, HALF, S)
         add_plane(nc.gpsimd, 1, 0, GPSIMD_CELLS)
-        first_product(3, 0, (HALF,), on_scalar)
         scatter_on_scalar(3, 0, HALF)
         first_product(3, HALF, (HALF,), on_scalar)
         scatter_on_scalar(3, HALF, S)
@@ -236,17 +236,17 @@ def tile_picked_unet_none_e_kernel(
         add_plane(nc.vector, 2, 0, FIRST_CELLS)
         add_plane(nc.vector, 2, FIRST_CELLS, U)
         add_chunks(3, 0, 0)
+        add_chunks(3, 2, 2)
         add_chunks(3, 1, 1)
-        weave(0, 0, on_vector)
-        weave(1, 1, on_scalar)
-        add_chunks(3, 2, 3)
+        weave(0, 0, on_scalar)
+        weave(2, 2, on_scalar)
+        add_chunks(3, 3, 5)
+        weave(1, 1, on_vector)
         sums0 = second_product(0, 1)
-        weave(3, 3, on_scalar)
-        weave(2, 2, on_vector)
+        sums1 = second_product(1, 2)
+        weave(3, 3, on_vector)
         unload(0, sums0, on_scalar)
         store(0, both)
-        sums1 = second_product(1, 2)
-        add_chunks(3, 4, 5)
         sums2 = second_product(2, 2)
         weave(4, 5, on_vector)
         unload(1, sums1, on_scalar, on_scalar)
@@ -256,9 +256,9 @@ def tile_picked_unet_none_e_kernel(
         sums5 = second_product(5, 2)
         unload(2, sums2, on_scalar, on_scalar)
         store_by_tile(2)
-        unload(3, sums3, on_scalar)
+        unload(3, sums3, on_vector)
         store(3, both)
-        unload(4, sums4, on_vector)
+        unload(4, sums4, on_scalar)
         store(4, both)
         unload(5, sums5, on_scalar, on_vector)
         store(5, both)

@@ -28,8 +28,6 @@ FIRST_POINTS = 128
 VECTOR_POINTS = 384
 W1_VECTOR_PAIRS = 40
 CELL_CHUNKS = (128, 256, 256, 128, 128, 128)
-GPSIMD_CELLS = 192
-FIRST_CELLS = 256
 WALK = 4
 
 
@@ -64,12 +62,11 @@ def tile_picked_unet_none_e_kernel(
             )
 
         skip_rows = skip.rearrange("(p t) v -> p t v", t=PACK)
-        skip1_start = U + FIRST_CELLS // 2 - GPSIMD_CELLS
-        sum_words = keep.tile([P, skip1_start + 2 * U], F32, name="sum_words")
+        sum_words = keep.tile([P, 2 * U + U // 2], F32, name="sum_words")
         skip_sb = {}
-        for t in (3, 2, 0, 1):
-            if t in (1, 2):
-                plane = sum_words[:, skip1_start + (t - 1) * U : skip1_start + t * U]
+        for t in (3, 2, 1, 0):
+            if t < 2:
+                plane = sum_words[:, U // 2 + t * U : U // 2 + (t + 1) * U]
             else:
                 plane = keep.tile([P, U], F32, name="skip_sb%d" % t)[:]
             nc.sync.dma_start(plane, skip_rows[:, t, :])
@@ -171,11 +168,10 @@ def tile_picked_unet_none_e_kernel(
         scatter_on_vector(2, 0, S)
         first_product(3, 0, (HALF,), on_scalar)
         scatter_on_scalar(1, HALF, S)
-        add_plane(nc.gpsimd, 1, 0, GPSIMD_CELLS)
         scatter_on_scalar(3, 0, HALF)
         first_product(3, HALF, (HALF,), on_scalar)
         scatter_on_scalar(3, HALF, S)
-        add_plane(nc.vector, 1, GPSIMD_CELLS, U)
+        add_plane(nc.vector, 1, 0, U)
 
         starts = [sum(CELL_CHUNKS[:c]) for c in range(len(CELL_CHUNKS))]
         chunks = [slice(start, start + width) for start, width in zip(starts, CELL_CHUNKS)]
@@ -233,8 +229,7 @@ def tile_picked_unet_none_e_kernel(
 
         both = slice(0, OUT_TILES)
 
-        add_plane(nc.vector, 2, 0, FIRST_CELLS)
-        add_plane(nc.vector, 2, FIRST_CELLS, U)
+        add_plane(nc.vector, 2, 0, U)
         add_chunks(3, 0, 0)
         add_chunks(3, 2, 2)
         add_chunks(3, 1, 1)

@@ -23,6 +23,7 @@ LIST_ROWS = 16
 QUADRANT = 32
 OUT_TILES = N // P
 HALF = S // 2
+DMA_ALIGN = 256
 
 FIRST_POINTS = 128
 VECTOR_POINTS = 384
@@ -42,18 +43,18 @@ def tile_picked_unet_none_e_kernel(
         offs_sb = keep.tile([P, S // LIST_ROWS], U16, name="offs_sb")
         cell_sb = keep.tile([P, S // LIST_ROWS], U16, name="cell_sb")
         x_rows = xT.rearrange("(p j) t -> p j t", j=PACK)
-        x_raw = [keep.tile([P, T], F32, name="x_raw%d" % j) for j in range(PACK)]
+        x_raw = [keep.tile([P, T], F32, name="x_raw%d" % j, align_bytes=DMA_ALIGN) for j in range(PACK)]
         nc.sync.dma_start(x_raw[0][:], x_rows[:, 0, :])
         nc.sync.dma_start(offs_sb[:], offs)
         for j in range(1, PACK):
             nc.sync.dma_start(x_raw[j][:], x_rows[:, j, :])
-        w1_raw = keep.tile([P, PACK, H], F32, name="w1_raw")
+        w1_raw = keep.tile([P, PACK, H], F32, name="w1_raw", align_bytes=DMA_ALIGN)
         nc.sync.dma_start(w1_raw[:], w1.rearrange("(p j) c -> p j c", j=PACK))
         nc.sync.dma_start(cell_sb[:], cell)
 
-        w2_codes = keep.tile([P, N], I32, name="w2_codes", align_bytes=64)
+        w2_codes = keep.tile([P, N], I32, name="w2_codes", align_bytes=DMA_ALIGN)
         nc.sync.dma_start(w2_codes[:], w2_words[0].rearrange("p n r -> p (n r)").bitcast(I32))
-        w2_sc = keep.tile([P, N], U8, name="w2_sc", align_bytes=64)
+        w2_sc = keep.tile([P, N], U8, name="w2_sc", align_bytes=DMA_ALIGN)
         nc.vector.memset(w2_sc[:].bitcast(I32), 0)
         for q in range(P // QUADRANT):
             nc.sync.dma_start(
@@ -62,13 +63,13 @@ def tile_picked_unet_none_e_kernel(
             )
 
         skip_rows = skip.rearrange("(p t) v -> p t v", t=PACK)
-        sum_words = keep.tile([P, 2 * U + U // 2], F32, name="sum_words")
+        sum_words = keep.tile([P, 2 * U + U // 2], F32, name="sum_words", align_bytes=DMA_ALIGN)
         skip_sb = {}
         for t in (3, 2, 1, 0):
             if t < 2:
                 plane = sum_words[:, U // 2 + t * U : U // 2 + (t + 1) * U]
             else:
-                plane = keep.tile([P, U], F32, name="skip_sb%d" % t)[:]
+                plane = keep.tile([P, U], F32, name="skip_sb%d" % t, align_bytes=DMA_ALIGN)[:]
             nc.sync.dma_start(plane, skip_rows[:, t, :])
             skip_sb[t] = plane
 
@@ -176,7 +177,7 @@ def tile_picked_unet_none_e_kernel(
         starts = [sum(CELL_CHUNKS[:c]) for c in range(len(CELL_CHUNKS))]
         chunks = [slice(start, start + width) for start, width in zip(starts, CELL_CHUNKS)]
         out_rows = out.rearrange("(g p) v -> p g v", p=P)
-        res = keep.tile([P, OUT_TILES, U], F32, name="res")
+        res = keep.tile([P, OUT_TILES, U], F32, name="res", align_bytes=DMA_ALIGN)
         z_bf = keep.tile([P, U * PACK], BF16, name="z_bf", align_bytes=64)
         weave_src = sums.rearrange("p (t c i) -> p c t i", t=PACK, i=WALK)
         weave_dst = z_bf[:].rearrange("p (c i t) -> p c t i", t=PACK, i=WALK)

@@ -26,7 +26,6 @@ HALF = S // 2
 DMA_ALIGN = 256
 
 FIRST_POINTS = 128
-VECTOR_POINTS = 384
 W1_VECTOR_PAIRS = 40
 CELL_CHUNKS = (128, 256, 256, 128, 128, 128)
 WALK = 4
@@ -43,7 +42,8 @@ def tile_picked_unet_none_e_kernel(
         offs_sb = keep.tile([P, S // LIST_ROWS], U16, name="offs_sb")
         cell_sb = keep.tile([P, S // LIST_ROWS], U16, name="cell_sb")
         x_rows = xT.rearrange("(p j) t -> p j t", j=PACK)
-        x_raw = [keep.tile([P, T], F32, name="x_raw%d" % j, align_bytes=DMA_ALIGN) for j in range(PACK)]
+        x_raw = [keep.tile([P, T], F32, name="x_raw%d" % j, align_bytes=DMA_ALIGN) for j in range(PACK - 1)]
+        x_raw.append(keep.tile([P, T], F32, name="x_last", tag="x_last", align_bytes=DMA_ALIGN))
         nc.sync.dma_start(x_raw[0][:], x_rows[:, 0, :])
         nc.sync.dma_start(offs_sb[:], offs)
         for j in range(1, PACK):
@@ -62,17 +62,6 @@ def tile_picked_unet_none_e_kernel(
                 w2_scales[0, 4 * q : 4 * q + 4, :].bitcast(I32),
             )
 
-        skip_rows = skip.rearrange("(p t) v -> p t v", t=PACK)
-        sum_words = keep.tile([P, 2 * U + U // 2], F32, name="sum_words", align_bytes=DMA_ALIGN)
-        skip_sb = {}
-        for t in (3, 2, 1, 0):
-            if t < 2:
-                plane = sum_words[:, U // 2 + t * U : U // 2 + (t + 1) * U]
-            else:
-                plane = keep.tile([P, U], F32, name="skip_sb%d" % t, align_bytes=DMA_ALIGN)[:]
-            nc.sync.dma_start(plane, skip_rows[:, t, :])
-            skip_sb[t] = plane
-
         up = []
         for t in range(PACK):
             window = keep.tile([P, U], F32, name="up%d" % t)
@@ -83,15 +72,19 @@ def tile_picked_unet_none_e_kernel(
             return list_sb[:, start // LIST_ROWS : stop // LIST_ROWS]
 
         x_bf = keep.tile([P, S, PACK], BF16, name="x_bf", align_bytes=64)
-        x_late = keep.tile([P, PACK, S - VECTOR_POINTS], BF16, name="x_late")
         for j in range(PACK):
-            nc.vector.tensor_copy(x_bf[:, :VECTOR_POINTS, j], x_raw[j][:].indirect(entries(offs_sb, 0, VECTOR_POINTS)))
-            nc.scalar.activation(x_late[:, j, :], x_raw[j][:].indirect(entries(offs_sb, VECTOR_POINTS, S)), COPY)
-            if j % 2:
-                nc.scalar.copy(x_bf[:, VECTOR_POINTS:, j - 1 : j + 1], x_late[:, j - 1 : j + 1, :].rearrange("p e s -> p s e"))
+            nc.vector.tensor_copy(x_bf[:, :HALF, j], x_raw[j][:].indirect(entries(offs_sb, 0, HALF)))
+            nc.scalar.activation(x_bf[:, HALF:, j], x_raw[j][:].indirect(entries(offs_sb, HALF, S)), COPY)
+        skip_rows = skip.rearrange("(p t) v -> p t v", t=PACK)
+        sum_words = keep.tile([P, PACK * U + U // 2], F32, name="sum_words", tag="x_last", align_bytes=DMA_ALIGN)
+        skip_sb = {}
+        for t in (3, 2, 1, 0):
+            skip_sb[t] = sum_words[:, U // 2 + t * U : U // 2 + (t + 1) * U]
+            nc.sync.dma_start(skip_sb[t], skip_rows[:, t, :])
+
         x_codes = keep.tile([P, S], U32, name="x_codes", align_bytes=64)
         x_sc = keep.tile([P, S], U8, name="x_sc", align_bytes=64)
-        for points in (slice(VECTOR_POINTS, S), slice(0, VECTOR_POINTS)):
+        for points in (slice(HALF, S), slice(0, HALF)):
             nc.vector.quantize_mx(
                 out=x_codes[:, points].bitcast(FP8X4),
                 scales=x_sc[:, points],
@@ -167,11 +160,10 @@ def tile_picked_unet_none_e_kernel(
         first_product(1, HALF, (HALF,), on_scalar)
         first_product(2, HALF, (HALF,), on_scalar)
         scatter_on_vector(2, 0, S)
-        first_product(3, 0, (HALF,), on_scalar)
+        first_product(3, 0, (S,), on_scalar)
+        scatter_on_scalar(3, 0, FIRST_POINTS)
         scatter_on_scalar(1, HALF, S)
-        scatter_on_scalar(3, 0, HALF)
-        first_product(3, HALF, (HALF,), on_scalar)
-        scatter_on_scalar(3, HALF, S)
+        scatter_on_scalar(3, FIRST_POINTS, S)
         add_plane(nc.vector, 1, 0, U)
 
         starts = [sum(CELL_CHUNKS[:c]) for c in range(len(CELL_CHUNKS))]

@@ -216,37 +216,39 @@ def tile_picked_unet_none_e_kernel(
         def store(c, tiles):
             nc.sync.dma_start(out_rows[:, tiles, chunks[c]], res[:, tiles, chunks[c]])
 
-        def store_by_tile(c):
-            for g in range(OUT_TILES):
-                store(c, slice(g, g + 1))
+        def unload_tile(c, parts, g, move):
+            move(res[:, g : g + 1, chunks[c]], parts[g])
+            store(c, slice(g, g + 1))
 
         both = slice(0, OUT_TILES)
 
         add_plane(nc.vector, 2, 0, U)
         add_chunks(3, 0, 0)
-        add_chunks(3, 2, 2)
         add_chunks(3, 1, 1)
         weave(0, 0, on_scalar)
+        add_chunks(3, 2, 2)
         weave(2, 2, on_scalar)
-        add_chunks(3, 3, 5)
         weave(1, 1, on_vector)
         sums0 = second_product(0, 1)
         sums1 = second_product(1, 2)
-        weave(3, 3, on_vector)
+        add_chunks(3, 3, 3)
+        add_chunks(3, 4, 5)
         unload(0, sums0, on_scalar)
         store(0, both)
+        weave(3, 3, on_vector)
+        unload_tile(1, sums1, 0, on_scalar)
+        unload_tile(1, sums1, 1, on_scalar)
         sums2 = second_product(2, 2)
-        weave(4, 5, on_vector)
-        unload(1, sums1, on_scalar, on_scalar)
-        store_by_tile(1)
+        weave(4, 4, on_vector)
         sums3 = second_product(3, 1)
-        sums4 = second_product(4, 1)
+        weave(5, 5, on_vector)
+        sums4 = second_product(4, 2)
         sums5 = second_product(5, 2)
-        unload(2, sums2, on_scalar, on_scalar)
-        store_by_tile(2)
-        unload(3, sums3, on_vector)
+        unload_tile(2, sums2, 0, on_scalar)
+        unload_tile(2, sums2, 1, on_scalar)
+        unload(3, sums3, on_scalar)
         store(3, both)
-        unload(4, sums4, on_scalar)
+        unload(4, sums4, on_scalar, on_vector)
         store(4, both)
         unload(5, sums5, on_scalar, on_vector)
         store(5, both)

@@ -27,7 +27,7 @@ DMA_ALIGN = 256
 
 FIRST_POINTS = 128
 W1_VECTOR_PAIRS = 40
-CELL_CHUNKS = (128, 256, 256, 128, 128, 128)
+CELL_CHUNKS = (128, 256, 128, 128, 128, 128, 128)
 WALK = 4
 
 
@@ -226,29 +226,33 @@ def tile_picked_unet_none_e_kernel(
         add_chunks(3, 0, 0)
         add_chunks(3, 1, 1)
         weave(0, 0, on_scalar)
-        add_chunks(3, 2, 2)
+        add_chunks(3, 2, 3)
         weave(2, 2, on_scalar)
+        weave(3, 3, on_scalar)
+        add_chunks(3, 4, 4)
         weave(1, 1, on_vector)
         sums0 = second_product(0, 1)
+        add_chunks(3, 5, 6)
         sums1 = second_product(1, 2)
-        add_chunks(3, 3, 3)
-        add_chunks(3, 4, 5)
+        sums2 = second_product(2, 1)
         unload(0, sums0, on_scalar)
         store(0, both)
-        weave(3, 3, on_vector)
-        unload_tile(1, sums1, 0, on_scalar)
-        unload_tile(1, sums1, 1, on_scalar)
-        sums2 = second_product(2, 2)
         weave(4, 4, on_vector)
         sums3 = second_product(3, 1)
+        unload_tile(1, sums1, 0, on_scalar)
+        unload_tile(1, sums1, 1, on_scalar)
         weave(5, 5, on_vector)
-        sums4 = second_product(4, 2)
-        sums5 = second_product(5, 2)
-        unload_tile(2, sums2, 0, on_scalar)
-        unload_tile(2, sums2, 1, on_scalar)
+        sums4 = second_product(4, 1)
+        weave(6, 6, on_vector)
+        sums5 = second_product(5, 1)
+        sums6 = second_product(6, 2)
+        unload(2, sums2, on_scalar)
+        store(2, both)
         unload(3, sums3, on_scalar)
         store(3, both)
-        unload(4, sums4, on_scalar, on_vector)
+        unload(4, sums4, on_scalar)
         store(4, both)
-        unload(5, sums5, on_scalar, on_vector)
+        unload(5, sums5, on_vector)
         store(5, both)
+        unload(6, sums6, on_scalar, on_vector)
+        store(6, both)

@@ -29,6 +29,7 @@ FIRST_POINTS = 128
 W1_VECTOR_PAIRS = 40
 CELL_CHUNKS = (128, 256, 128, 128, 128, 128, 128)
 WALK = 4
+VECTOR_ENTRIES = 384
 
 
 def tile_picked_unet_none_e_kernel(
@@ -67,6 +68,9 @@ def tile_picked_unet_none_e_kernel(
             window = keep.tile([P, U], F32, name="up%d" % t)
             nc.vector.memset(window[:], 0.0)
             up.append(window)
+
+        one = keep.tile([P, 1], F32, name="one")
+        nc.vector.memset(one[:], 1.0)
 
         def entries(list_sb, start, stop):
             return list_sb[:, start // LIST_ROWS : stop // LIST_ROWS]
@@ -154,16 +158,16 @@ def tile_picked_unet_none_e_kernel(
         first_product(1, 0, (HALF,), on_scalar)
         first_product(0, FIRST_POINTS, (FIRST_POINTS, HALF), on_scalar)
         scatter_on_scalar(1, 0, HALF)
-        first_product(2, 0, (HALF,), on_vector)
+        first_product(2, 0, (HALF, FIRST_POINTS), on_vector)
         scatter_on_vector(0, FIRST_POINTS, S)
         add_plane(nc.gpsimd, 0, 0, U)
+        first_product(2, VECTOR_ENTRIES, (FIRST_POINTS,), on_scalar)
         first_product(1, HALF, (HALF,), on_scalar)
-        first_product(2, HALF, (HALF,), on_scalar)
-        scatter_on_vector(2, 0, S)
-        first_product(3, 0, (S,), on_scalar)
-        scatter_on_scalar(3, 0, FIRST_POINTS)
+        scatter_on_scalar(2, VECTOR_ENTRIES, S)
+        first_product(3, 0, (S,), on_vector)
+        scatter_on_vector(2, 0, VECTOR_ENTRIES)
         scatter_on_scalar(1, HALF, S)
-        scatter_on_scalar(3, FIRST_POINTS, S)
+        nc.scalar.activation(up[3][:].indirect(cell_sb[:]), h[3][:], COPY, scale=one[:])
         add_plane(nc.vector, 1, 0, U)
 
         starts = [sum(CELL_CHUNKS[:c]) for c in range(len(CELL_CHUNKS))]

from contextlib import ExitStack

import concourse.mybir as mybir

K, T, S, H, N, U = 512, 2048, 512, 512, 256, 1024
FLOPS = 2 * K * H * S + 2 * H * N * U

F32 = mybir.dt.float32
BF16 = mybir.dt.bfloat16
I32 = mybir.dt.int32
U32 = mybir.dt.uint32
U16 = mybir.dt.uint16
U8 = mybir.dt.uint8
FP8X4 = mybir.dt.float8_e4m3fn_x4
ADD = mybir.AluOpType.add
COPY = mybir.ActivationFunctionType.Copy

P = 128
PACK = 4
BANK = 512
BANKS = 8
LIST_ROWS = 16
QUADRANT = 32
OUT_TILES = N // P
HALF = S // 2
DMA_ALIGN = 256

FIRST_POINTS = 128
W1_VECTOR_PAIRS = 40
CELL_CHUNKS = (128, 256, 128, 128, 128, 128, 128)
WALK = 4
VECTOR_ENTRIES = 384


def tile_picked_unet_none_e_kernel(
    tc, xT, w1, w2_words, w2_scales, skip, offs, cell, out
):
    nc = tc.nc
    with ExitStack() as ctx:
        keep = ctx.enter_context(tc.tile_pool(name="keep", bufs=1))
        psum = ctx.enter_context(tc.psum_pool(name="psum", bufs=BANKS))

        offs_sb = keep.tile([P, S // LIST_ROWS], U16, name="offs_sb")
        cell_sb = keep.tile([P, S // LIST_ROWS], U16, name="cell_sb")
        x_rows = xT.rearrange("(p j) t -> p j t", j=PACK)
        x_raw = [keep.tile([P, T], F32, name="x_raw%d" % j, align_bytes=DMA_ALIGN) for j in range(PACK - 1)]
        x_raw.append(keep.tile([P, T], F32, name="x_last", tag="x_last", align_bytes=DMA_ALIGN))
        nc.sync.dma_start(x_raw[0][:], x_rows[:, 0, :])
        nc.sync.dma_start(offs_sb[:], offs)
        for j in range(1, PACK):
            nc.sync.dma_start(x_raw[j][:], x_rows[:, j, :])
        w1_raw = keep.tile([P, PACK, H], F32, name="w1_raw", align_bytes=DMA_ALIGN)
        nc.sync.dma_start(w1_raw[:], w1.rearrange("(p j) c -> p j c", j=PACK))
        nc.sync.dma_start(cell_sb[:], cell)

        w2_codes = keep.tile([P, N], I32, name="w2_codes", align_bytes=DMA_ALIGN)
        nc.sync.dma_start(w2_codes[:], w2_words[0].rearrange("p n r -> p (n r)").bitcast(I32))
        w2_sc = keep.tile([P, N], U8, name="w2_sc", align_bytes=DMA_ALIGN)
        nc.vector.memset(w2_sc[:].bitcast(I32), 0)
        for q in range(P // QUADRANT):
            nc.sync.dma_start(
                w2_sc[QUADRANT * q : QUADRANT * q + 4, :].bitcast(I32),
                w2_scales[0, 4 * q : 4 * q + 4, :].bitcast(I32),
            )

        up = []
        for t in range(PACK):
            window = keep.tile([P, U], F32, name="up%d" % t)
            nc.vector.memset(window[:], 0.0)
            up.append(window)

        one = keep.tile([P, 1], F32, name="one")
        nc.vector.memset(one[:], 1.0)

        def entries(list_sb, start, stop):
            return list_sb[:, start // LIST_ROWS : stop // LIST_ROWS]

        x_bf = keep.tile([P, S, PACK], BF16, name="x_bf", align_bytes=64)
        for j in range(PACK):
            nc.vector.tensor_copy(x_bf[:, :HALF, j], x_raw[j][:].indirect(entries(offs_sb, 0, HALF)))
            nc.scalar.activation(x_bf[:, HALF:, j], x_raw[j][:].indirect(entries(offs_sb, HALF, S)), COPY)
        skip_rows = skip.rearrange("(p t) v -> p t v", t=PACK)
        sum_words = keep.tile([P, PACK * U + U // 2], F32, name="sum_words", tag="x_last", align_bytes=DMA_ALIGN)
        skip_sb = {}
        for t in (3, 2, 1, 0):
            skip_sb[t] = sum_words[:, U // 2 + t * U : U // 2 + (t + 1) * U]
            nc.sync.dma_start(skip_sb[t], skip_rows[:, t, :])

        x_codes = keep.tile([P, S], U32, name="x_codes", align_bytes=64)
        x_sc = keep.tile([P, S], U8, name="x_sc", align_bytes=64)
        for points in (slice(HALF, S), slice(0, HALF)):
            nc.vector.quantize_mx(
                out=x_codes[:, points].bitcast(FP8X4),
                scales=x_sc[:, points],
                in_=x_bf[:, points, :].rearrange("p s j -> p (s j)"),
            )

        w1_bf = keep.tile([P, H * PACK], BF16, name="w1_bf", align_bytes=64)
        w1_codes = keep.tile([P, H], U32, name="w1_codes", align_bytes=64)
        w1_sc = keep.tile([P, H], U8, name="w1_sc", align_bytes=64)
        w1_dst = w1_bf[:].rearrange("p (u e mm mi j) -> p u mm j mi e", u=2, e=2, mi=2, j=PACK)
        w1_src = w1_raw[:].rearrange("p j (mm mi u e) -> p u mm j mi e", mi=2, u=2, e=2)
        w1_dst3 = w1_bf[:].rearrange("p (u e m j) -> p u m j e", u=2, e=2, j=PACK)
        w1_src3 = w1_raw[:].rearrange("p j (m u e) -> p u m j e", u=2, e=2)

        def round_w1(u):
            nc.vector.tensor_copy(w1_dst[:, u, :W1_VECTOR_PAIRS], w1_src[:, u, :W1_VECTOR_PAIRS])
            nc.scalar.activation(w1_dst3[:, u, 2 * W1_VECTOR_PAIRS :], w1_src3[:, u, 2 * W1_VECTOR_PAIRS :], COPY)

        def quantize_w1(t_from, t_to):
            nc.vector.quantize_mx(
                out=w1_codes[:, t_from * P : t_to * P].bitcast(FP8X4),
                scales=w1_sc[:, t_from * P : t_to * P],
                in_=w1_bf[:, t_from * P * PACK : t_to * P * PACK],
            )

        round_w1(0)
        quantize_w1(0, 1)
        quantize_w1(1, 2)
        round_w1(1)
        quantize_w1(2, 4)

        h = [keep.tile([P, S], F32, name="h%d" % t) for t in range(PACK)]
        on_vector, on_scalar = nc.vector.tensor_copy, nc.scalar.copy

        def first_product(t, start, widths, move):
            bank = psum.tile([P, BANK], F32, name="bank")
            done = 0
            for width in widths:
                points = slice(start + done, start + done + width)
                nc.tensor.matmul_mx(
                    out=bank[:, done : done + width],
                    lhsT=w1_codes[:, t * P : (t + 1) * P].bitcast(FP8X4),
                    lhsT_scale=w1_sc[:, t * P : (t + 1) * P],
                    rhs=x_codes[:, points].bitcast(FP8X4),
                    rhs_scale=x_sc[:, points],
                    start=True,
                    stop=True,
                )
                done = done + width
            move(h[t][:, start : start + done], bank[:, :done])

        def scatter_on_vector(t, start, stop):
            nc.vector.tensor_copy(up[t][:].indirect(entries(cell_sb, start, stop)), h[t][:, start:stop])

        def scatter_on_scalar(t, start, stop):
            nc.scalar.activation(up[t][:].indirect(entries(cell_sb, start, stop)), h[t][:, start:stop], COPY)

        sums = sum_words[:, : 2 * U].bitcast(BF16)

        def add_plane(engine, t, start, stop):
            engine.tensor_tensor(
                sums[:, t * U + start : t * U + stop], up[t][:, start:stop], skip_sb[t][:, start:stop], ADD
            )

        first_product(0, 0, (FIRST_POINTS,), on_scalar)
        scatter_on_vector(0, 0, FIRST_POINTS)
        first_product(1, 0, (HALF,), on_scalar)
        first_product(0, FIRST_POINTS, (FIRST_POINTS, HALF), on_scalar)
        scatter_on_scalar(1, 0, HALF)
        first_product(2, 0, (HALF, FIRST_POINTS), on_vector)
        scatter_on_vector(0, FIRST_POINTS, S)
        add_plane(nc.gpsimd, 0, 0, U)
        first_product(2, VECTOR_ENTRIES, (FIRST_POINTS,), on_scalar)
        first_product(1, HALF, (HALF,), on_scalar)
        scatter_on_scalar(2, VECTOR_ENTRIES, S)
        first_product(3, 0, (S,), on_vector)
        scatter_on_vector(2, 0, VECTOR_ENTRIES)
        scatter_on_scalar(1, HALF, S)
        nc.scalar.activation(up[3][:].indirect(cell_sb[:]), h[3][:], COPY, scale=one[:])
        add_plane(nc.vector, 1, 0, U)

        starts = [sum(CELL_CHUNKS[:c]) for c in range(len(CELL_CHUNKS))]
        chunks = [slice(start, start + width) for start, width in zip(starts, CELL_CHUNKS)]
        out_rows = out.rearrange("(g p) v -> p g v", p=P)
        res = keep.tile([P, OUT_TILES, U], F32, name="res", align_bytes=DMA_ALIGN)
        z_bf = keep.tile([P, U * PACK], BF16, name="z_bf", align_bytes=64)
        weave_src = sums.rearrange("p (t c i) -> p c t i", t=PACK, i=WALK)
        weave_dst = z_bf[:].rearrange("p (c i t) -> p c t i", t=PACK, i=WALK)

        def add_chunks(t, first, last):
            add_plane(nc.vector, t, chunks[first].start, chunks[last].stop)

        def weave(first, last, move):
            runs = slice(chunks[first].start // WALK, chunks[last].stop // WALK)
            move(weave_dst[:, runs], weave_src[:, runs])

        def second_product(c, banks):
            width = CELL_CHUNKS[c]
            z_codes = keep.tile([P, width], U32, name="z_codes%d" % c, align_bytes=64)
            z_sc = keep.tile([P, width], U8, name="z_sc%d" % c, align_bytes=64)
            nc.vector.quantize_mx(
                out=z_codes[:].bitcast(FP8X4),
                scales=z_sc[:],
                in_=z_bf[:, PACK * chunks[c].start : PACK * chunks[c].stop],
            )
            per_bank = OUT_TILES // banks
            parts = []
            for b in range(banks):
                bank = psum.tile([P, BANK], F32, name="bank")
                for place in range(per_bank):
                    g = b * per_bank + place
                    nc.tensor.matmul_mx(
                        out=bank[:, place * width : (place + 1) * width],
                        lhsT=w2_codes[:, g * P : (g + 1) * P].bitcast(FP8X4),
                        lhsT_scale=w2_sc[:, g * P : (g + 1) * P],
                        rhs=z_codes[:].bitcast(FP8X4),
                        rhs_scale=z_sc[:],
                        start=True,
                        stop=True,
                    )
                parts.append(bank[:, : per_bank * width].rearrange("p (g v) -> p g v", g=per_bank))
            return parts

        def unload(c, parts, *moves):
            per_bank = OUT_TILES // len(parts)
            for b, (bank_sums, move) in enumerate(zip(parts, moves)):
                move(res[:, b * per_bank : (b + 1) * per_bank, chunks[c]], bank_sums)

        def store(c, tiles):
            nc.sync.dma_start(out_rows[:, tiles, chunks[c]], res[:, tiles, chunks[c]])

        def unload_tile(c, parts, g, move):
            move(res[:, g : g + 1, chunks[c]], parts[g])
            store(c, slice(g, g + 1))

        both = slice(0, OUT_TILES)

        add_plane(nc.vector, 2, 0, U)
        add_chunks(3, 0, 0)
        add_chunks(3, 1, 1)
        weave(0, 0, on_scalar)
        add_chunks(3, 2, 3)
        weave(2, 2, on_scalar)
        weave(3, 3, on_scalar)
        add_chunks(3, 4, 4)
        weave(1, 1, on_vector)
        sums0 = second_product(0, 1)
        add_chunks(3, 5, 6)
        sums1 = second_product(1, 2)
        sums2 = second_product(2, 1)
        unload(0, sums0, on_scalar)
        store(0, both)
        weave(4, 4, on_vector)
        sums3 = second_product(3, 1)
        unload_tile(1, sums1, 0, on_scalar)
        unload_tile(1, sums1, 1, on_scalar)
        weave(5, 5, on_vector)
        sums4 = second_product(4, 1)
        weave(6, 6, on_vector)
        sums5 = second_product(5, 1)
        sums6 = second_product(6, 2)
        unload(2, sums2, on_scalar)
        store(2, both)
        unload(3, sums3, on_scalar)
        store(3, both)
        unload(4, sums4, on_scalar)
        store(4, both)
        unload(5, sums5, on_vector)
        store(5, both)
        unload(6, sums6, on_scalar, on_vector)
        store(6, both)
